import numpy as np, ml_dtypes
CORES = [25,29,65,69,153,157,193,197]
N = 8
import mx_ref
BF = ml_dtypes.bfloat16
def gentries(a):
    return np.ascontiguousarray(a.reshape(8, 16, -1).transpose(0, 2, 1)).reshape(8, -1)
def gtable(e):
    e = np.asarray(e); return np.ascontiguousarray(e.reshape(8, -1, 16).transpose(0, 2, 1)).reshape(128, -1).astype(np.int32)
def gcols(t, e):
    v = np.concatenate([t.reshape(8, 16, -1, 4), np.zeros((8, 16, 1, 4), BF)], axis=2)
    return np.ascontiguousarray(np.stack([v[g][:, e[g]] for g in range(8)])).reshape(128, -1)
def gpick(z, e):
    return np.concatenate([z[16 * g:16 * g + 16][:, e[g]] for g in range(8)])
def tile(rs):
    return np.stack(rs, axis=2).reshape(128, -1).astype(BF)
def pick(q, e):
    c = np.concatenate([q[0].reshape(128, -1, 4), np.zeros((128, 1, 4), np.uint8)], axis=1); s = np.concatenate([q[1], np.ones((16, 1), np.uint8)], axis=1)
    return (np.ascontiguousarray(c[:, e].reshape(128, -1)), np.ascontiguousarray(s[:, e]))
def join(*qs):
    return (np.concatenate([q[0] for q in qs], axis=1), np.concatenate([q[1] for q in qs], axis=1))
def put(q, e, v):
    c, s = q[0].reshape(128, -1, 4).copy(), q[1].copy(); c[:, e] = v[0].reshape(128, -1, 4); s[:, e] = v[1]
    return (c.reshape(128, -1), s)
def pk(c, s):
    return (np.ascontiguousarray(c), mx_ref.live(s))
def emit(q):
    return q[0], q[1]
def packed(v, rng):
    q = [mx_ref.quantize(np.ascontiguousarray(v[r])) for r in range(N)]
    return np.stack([a for a, b in q]), np.stack([mx_ref.plane(b, rng) for a, b in q])
def values_of_codes():
    e, c = np.zeros((128, 128, 4), np.float32), np.zeros((128, 2, 4), np.uint8)
    e[np.arange(128), np.arange(128), 0] = 1
    c[:127, :, 0] = np.arange(256).reshape(2, 128).T[:127]
    return mx_ref.matmul(mx_ref.quantize(e.reshape(128, 512).astype(BF)), (c.reshape(128, 8), np.full((16, 2), 127, np.uint8))).T.reshape(-1).astype(np.float64)
CODE_VALUE, SCALE_VALUE = values_of_codes(), 2.0 ** (np.arange(256) - 127.0)
def decode(q):
    return (CODE_VALUE[q[0]].reshape(16, 8, -1, 4) * SCALE_VALUE[q[1]][:, None, :, None] + 0.0).reshape(128, -1).astype(np.float32)
def f(rng, *shape):
    return mx_ref.flush((rng.standard_normal(shape, dtype=np.float32) * np.exp2(rng.integers(-2, 3, shape[:-1] + (1,)))).astype(BF))
def wide(rng, *shape, cols=0):
    v = rng.standard_normal(shape, dtype=np.float32) * np.exp2(rng.integers(-12, 13, shape)).astype(np.float32)
    if cols: v *= np.repeat(np.exp2(rng.integers(-cols, cols + 1, shape[:-2] + (1, shape[-1] // 4))) * (rng.random(shape[:-2] + (1, shape[-1] // 4)) > 0.0625), 4, axis=-1).astype(np.float32)
    return mx_ref.flush(v.astype(BF))
C = 288
STEP = [1, 4, 2]
def numbers_of(rng):
    return {"x": np.array(f(rng, N, 128, 4 * C)), "u": np.array(f(rng, N, 128, 512)), "v": np.array(f(rng, N, 128, 512))}
def orders(rng):
    return rng.permuted(np.tile(np.arange(C), (N, 8, 1)), axis=2)
def mates(rng):
    e = orders(rng)
    m = np.zeros_like(e)
    np.put_along_axis(m, e[:, :, 0::2], e[:, :, 1::2], axis=2)
    np.put_along_axis(m, e[:, :, 1::2], e[:, :, 0::2], axis=2)
    return m
def stored(c, a, m):
    return {"cl": np.stack([gtable(c[r]) for r in range(N)]), "pl": np.stack([gtable(a[r]) for r in range(N)]), "ml": np.stack([gtable(m[r]) for r in range(N)])}
def lists(rng):
    return stored(orders(rng), orders(rng), mates(rng))
def layers(rng, still=[]):
    w = np.array(f(rng, N, 128, 2048)).reshape(N, 8, 16, 4, 8, 16, 4)
    for i in still:
        w[:, :, i] = 0
        w[:, :, :, :, :, i] = 0
    return w
def weights(rng, w):
    c, s = packed(np.ascontiguousarray(w).reshape(N, 128, 2048), rng)
    return {"wc": c, "ws": s}
def setup_inputs(rng):
    return {**numbers_of(rng), **lists(rng), **weights(rng, layers(rng))}
def setup_inputs_ties(rng):
    d = numbers_of(rng)
    o = rng.permutation(N)
    k = rng.integers(0, 4, (N, 8, C))
    k[o[1]] -= 4
    k[o[2], rng.permutation(8)[:4]] = 1
    x = d["x"].reshape(N, 8, 16, C, 4)
    x[:, :, 0] = 0
    x[:, :, 0, :, 0] = k.astype(np.float32).astype(BF)
    u = d["u"].reshape(N, 128, 128, 4)
    u[:, :, ::16] = 0
    for r in range(N):
        for h in range(0, 128, 16): u[r, h, h, 0] = 0.0 if r == o[0] else 1.0
    c, a, m = orders(rng), orders(rng), mates(rng)
    c[o[3]] = m[o[3]]
    return {"x": x.reshape(N, 128, 4 * C), "u": u.reshape(N, 128, 512), "v": d["v"], **stored(c, a, m), **weights(rng, layers(rng, [0]))}
def setup_inputs_near(rng):
    d = numbers_of(rng)
    x = d["x"].astype(np.float32).reshape(N, 8, 16, C, 4)
    x[:, :, 0] = 0
    x[:, :, 8:] = 0
    u = d["u"].reshape(N, 128, 128, 4)
    u[:, :, ::16] = 0
    o = (np.arange(N) + rng.integers(4)) % 4
    for r in range(N):
        c = rng.choice([-1.0, 1.0], (8, 1))
        s = rng.integers(0, 16, (8, C))
        digits = ((s[:, :, None] >> np.arange(4)) & 1) * np.exp2(np.arange(4) - 23.0)
        if o[r] < 2:
            x[r, :, 0, :, 0] = c
            x[r, :, 8] = digits
            x[r, :, 11, :, 0] = 2.0 ** -10
        elif o[r] == 2: x[r, :, 8] = digits * rng.choice([-1.0, 1.0], (8, C, 1))
        else:
            x[r, :, 8, :, 0] = np.where(s < 8, 1.25, 0.0) * 2.0 ** -29 * c
            x[r, :, 9, :, 0] = np.where(s < 8, 0.0, 1.125) * 2.0 ** -29 * c
            for g in rng.permutation(8)[:4]:
                e = rng.choice([-1.0, 1.0], C) * 2.0 ** -29
                x[r, g, 8, :, 0] = 1.25 * e
                x[r, g, 9, :, 0] = -1.125 * e
        if o[r] >= 2: x[r, :, 12, :, 0] = np.where(rng.random((8, C)) < 0.5, 1.0, 1.5) * 2.0 ** -30
        at = [0, C - 1, int(rng.integers(C)), int(rng.integers(C))]
        for g, j in zip(rng.permutation(8)[:4], at): x[r, g, 0, j, 0] = 2.0 ** 29 * rng.choice([-1.0, 1.0])
        k = 1.0 if o[r] == 0 else 2.0 ** -30
        for h in range(0, 128, 16):
            u[r, h, h, 0] = k if o[r] < 2 else 1.0
            if o[r] < 2: u[r, h + 11, h, 0] = k
            if o[r] < 3: u[r, h + 8, h] = k
            else:
                u[r, h + 8, h, 0] = k
                u[r, h + 9, h, 0] = 1.125 * k
                u[r, h + 10, h, 0] = k
    w = layers(rng, [0, 8, 9, 10, 11, 12, 13, 14, 15])
    for g in range(8): w[:, g, 12, 0, g, 10, 0] = 2.0 ** -8
    return {"x": x.reshape(N, 128, 4 * C).astype(BF), "u": u.reshape(N, 128, 512), "v": d["v"], **lists(rng), **weights(rng, w)}
def setup_inputs_odd(rng):
    d = numbers_of(rng)
    k = (N, 8, 2, 8, C, 4)
    x = (1.0 + (2 * rng.integers(0, 64, k) + 1) * 2.0 ** -7) * np.exp2(-rng.integers(0, 7, k).astype(np.float64)) * rng.choice([-1.0, 1.0], k)
    x[:, :, 0, 0, :, 0] = 1.96875 * 2.0 ** 8 * rng.choice([-1.0, 1.0], (N, 8, C))
    x[:, :, 1, 0, :, 0] = np.where(rng.random((N, 8, C)) < 0.5, 1.875, 0.09375) * 2.0 ** 8
    u = d["u"].reshape(N, 8, 2, 8, 128, 4)
    u[:, :, :, 0, ::16] = 0
    for r in range(N):
        for i, g in enumerate(rng.permutation(8)[:4]):
            x[r, g, 0, 1, :, 0] = (8 + rng.integers(0, 2, C)) * 2.0 ** (i - 8)
            u[r, :, :, :, 16 * g] = 0
            u[r, g, 0, 1, 16 * g, 0] = 1.0
    return {"x": x.astype(np.float32).reshape(N, 128, 4 * C).astype(BF), "u": u.reshape(N, 128, 512), "v": d["v"], **lists(rng), **weights(rng, layers(rng, [0, 8]))}
def setup_inputs_ends(rng):
    d = numbers_of(rng)
    x = np.zeros((N, 8, 16, C, 4))
    u = d["u"].astype(np.float32).reshape(N, 128, 128, 4)
    v = d["v"].astype(np.float32)
    w = np.zeros((N, 128, 4, 128, 4), np.float32)
    o, e = rng.permutation(N) % 4, rng.permutation(N) % 4
    i = np.arange(128)
    for r in range(N):
        h = rng.permutation(8)
        s = np.where(h < 2, 0.0, h % 2 * 2.0 - 1.0)[None, :, None]
        high = (0.9 + 0.1 * rng.random((8, 16, C, 4))) * 2.0 ** 30
        if o[r] == 0: x[r] = -high
        if o[r] == 1: x[r] = high * rng.choice([-1.0, 1.0], (1, 1, C, 1))
        if o[r] == 2: x[r] = -(1.0 + 0.125 * rng.integers(0, 8, (8, 16, C, 4))) * 2.0 ** -30
        if o[r] == 3: x[r] = d["x"][r].astype(np.float32).reshape(8, 16, C, 4)[:, :, :1]
        if o[r] < 2:
            x[r, :, 15] = 0
            u[r, :, ::16] = s * (0.9 + 0.1 * rng.random((128, 8, 4))) * 2.0 ** 30
            v[r] = rng.choice([-1.0, 1.0], (128, 512)) * (0.9 + 0.1 * rng.random((128, 512))) * 2.0 ** 30
        if o[r] == 2:
            u[r, :, ::16] = s * (1.0 + 0.125 * rng.integers(0, 8, (128, 8, 4))) * 2.0 ** -30
            v[r] = rng.choice([-1.0, 1.0], (128, 512)) * (1.0 + 0.125 * rng.integers(0, 8, (128, 512))) * 2.0 ** -30
        if o[r] == 3: u[r, :, ::16] *= np.abs(s).astype(np.float32)
        k = np.full(128, [-0.125, -0.125, 0.25, 2.0 ** -8][o[r]])
        if o[r] >= 2: k[15::16] = 2.0 ** 8
        for b in range(4): w[r, i, b, i, b] = k
    c, a, m = orders(rng), orders(rng), mates(rng)
    j = np.arange(C)
    c[e == 0], m[e == 0] = j, j ^ 1
    c[e == 1], m[e == 1] = C - 1 - j, C - 1 - j
    c[e == 2], a[e == 2], m[e == 2] = C - 1 - j, j, (j + C // 2) % C
    return {"x": x.astype(np.float32).reshape(N, 128, 4 * C).astype(BF), "u": u.reshape(N, 128, 512).astype(BF), "v": v.astype(BF), **stored(c, a, m), **weights(rng, w.astype(BF))}
def setup_inputs_spread(rng):
    d = setup_inputs(rng)
    d["x"] = wide(rng, N, 128, 4 * C, cols=6)
    return d
def check_inputs(d):
    b = []
    for k in ("x", "u", "v"):
        a = np.abs(d[k].astype(np.float32))
        if not (np.isfinite(a).all() and ((a == 0) | (a >= 2.0 ** -30) & (a <= 2.0 ** 30)).all()): b.append("a value of " + k)
    j = np.arange(C)
    for k in ("cl", "pl", "ml"):
        for r in range(N):
            e = gentries(d[k][r])
            if not (np.sort(e, axis=1) == j).all(): b.append("a list of " + k)
            elif k == "ml" and ((at(e, e) != j) | (e == j)).any(): b.append("ml: mates")
    none, least, most = [emit(mx_ref.quantize(np.full((128, 16), k, np.float32).astype(BF)))[1][0, 0] for k in (0.0, 2.0 ** -8, 2.0 ** 8)]
    for r in range(N):
        if ((d["wc"][r] == 0x7F) | (d["wc"][r] == 0xFF)).any(): b.append("wc: a code that is no number")
        s = mx_ref.live(d["ws"][r])
        if ((s != none) & ((s < least) | (s > most))).any(): b.append("ws: a scale out of range")
        if (((d["wc"][r].reshape(16, 8, 512, 4) & 0x7F) != 0) & (s == none)[:, None, :, None]).any(): b.append("wc: a code other than zero under the scale of zeros")
    return b
def at(a, e):
    return np.take_along_axis(a, e, axis=1)
def above(s, a, b):
    return (at(s, a) > at(s, b)) | (at(s, a) == at(s, b)) & (a < b)
def reference(x, u, v, cl, pl, ml, wc, ws):
    qu = [mx_ref.quantize(u[r]) for r in range(N)]
    lay = [pk(wc[r], ws[r]) for r in range(N)]
    child, parent, mate = [gentries(cl[r]) for r in range(N)], [gentries(pl[r]) for r in range(N)], [gentries(ml[r]) for r in range(N)]
    j = np.tile(np.arange(C), (8, 1))
    now = [x[r] for r in range(N)]
    for step in STEP:
        t, z = [], []
        for r in range(N):
            q = mx_ref.quantize(now[r])
            s = mx_ref.matmul(qu[r], q)[::16] + np.float32(0.0)
            c, m = child[r], mate[r]
            o = np.where(above(s, j, m) == above(s, c, at(c, m)), c, at(c, m))
            new = np.argsort(o, axis=1)
            k = at(o, at(np.argsort(parent[r], axis=1), at(m, at(parent[r], new))))
            t.append(decode(q))
            p = t[r].astype(BF)
            z.append(mx_ref.quantize(((gcols(p, new).astype(np.float32) + gcols(p, k).astype(np.float32)) * np.float32(0.5)).astype(BF)))
            parent[r], mate[r] = new, k
        for r in range(N):
            h = [mx_ref.matmul(pick(lay[r], np.arange(128 * b, 128 * b + 128)), z[(r - step) % N]) * np.float32(0.03125) for b in range(4)]
            now[r] = tile([t[r][:, b::4] + gpick(h[b], parent[r]) for b in range(4)])
    y, co = np.zeros((N, 128, C), np.float32), np.zeros((N, 8, C), np.float32)
    oc, osc = np.zeros((N, 128, 4 * C), np.uint8), np.zeros((N, 16, C), np.uint8)
    for r in range(N):
        q = mx_ref.quantize(now[r])
        y[r] = mx_ref.matmul(mx_ref.quantize(v[r]), q)
        co[r] = mate[r]
        oc[r], osc[r] = emit(q)
    return {"y": y, "co": co, "oc": oc, "osc": osc}

@@ -1,0 +1,505 @@
+from concourse.bass import DstId, RemoteDMATransfer
+from concourse.mybir import dt, AluOpType, ActivationFunctionType
+
+N = 8
+C = 288
+H = C // 2
+K = C // 16
+STEP = [1, 4, 2]
+WORLD = 256
+BIG, BIGF = float(2 ** 20), 4.0
+A = AluOpType
+COPY = ActivationFunctionType.Copy
+
+SCRATCH = {
+    "li": ("sbuf", [128, 3 * K], "int32"), "lu": ("sbuf", [128, 3 * K], "uint16"),
+    "pc": ("sbuf", [128, 2], "int32"), "off": ("sbuf", [128, 4], "float32"), "iw": ("sbuf", [128, K], "float32"),
+    "dd": ("sbuf", [128, C], "int32"), "c32": ("sbuf", [128, 3 * C], "float32"), "c16": ("sbuf", [128, 2 * C], "bfloat16"),
+    "io_f": ("sbuf", [128, C], "float32"), "kt": ("sbuf", [128, 2 * C], "float32"),
+    "rr": ("sbuf", [128, 60 * C], "float32"), "rb": ("sbuf", [128, 30 * C], "bfloat16"),
+    "wf": ("sbuf", [128, 150 * K], "float32"), "wi": ("sbuf", [128, 50 * K], "int32"), "wu": ("sbuf", [128, 40 * K], "uint16"),
+    "kr": ("sbuf", [128, C], "float32"),
+    "eb": ("sbuf", [128, 520], "bfloat16"), "eq": ("sbuf", [128, 512], "float8_e4m3fn_x4"), "es": ("sbuf", [128, 512], "uint8"),
+    "uo_i": ("sbuf", [128, 8], "int32"), "uo": ("sbuf", [128, 8], "uint16"),
+    "ut": ("sbuf", [128, 512], "bfloat16"), "uq": ("sbuf", [128, 128], "float8_e4m3fn_x4"), "us": ("sbuf", [128, 128], "uint8"),
+    "pq": ("sbuf", [128, 128], "float8_e4m3fn_x4"), "pl_s": ("sbuf", [128, 128], "uint8"),
+    "vt": ("sbuf", [128, 512], "bfloat16"), "vq": ("sbuf", [128, 128], "float8_e4m3fn_x4"), "vs": ("sbuf", [128, 128], "uint8"),
+    "wq": ("sbuf", [128, 512], "float8_e4m3fn_x4"), "wp": ("sbuf", [128, 512], "uint8"),
+    "yo": ("sbuf", [128, C], "float32"),
+    "pa": ("psum", [128, 2048], "float32"), "pb": ("psum", [128, 1024], "float32"), "pz": ("psum", [128, 1024], "float32"),
+}
+SEMAPHORES = ["sv", "ss", "sp", "sg", "dl", "du", "dx", "dw", "dv", "dy", "dz", "ls"]
+for _n in range(4):
+    SCRATCH["x%d" % _n] = ("sbuf", [128, 4 * C], "bfloat16")
+    SCRATCH["q%d" % _n] = ("sbuf", [128, C], "float8_e4m3fn_x4")
+    SCRATCH["s%d" % _n] = ("sbuf", [128, C], "uint8")
+for _n in range(3):
+    SCRATCH["lq%d" % _n] = ("sbuf", [128, C], "float8_e4m3fn_x4")
+    SCRATCH["lp%d" % _n] = ("sbuf", [128, C], "uint8")
+    SCRATCH["hq%d" % _n] = ("sbuf", [128, H], "float8_e4m3fn_x4")
+    SCRATCH["hp%d" % _n] = ("sbuf", [128, H], "uint8")
+    for _k in "ak":
+        SCRATCH["o%s%d" % (_k, _n)] = ("sbuf", [128, 2 * K if _k == "a" else K], "uint16")
+        SCRATCH["l%s%d" % (_k, _n)] = ("sbuf", [128, K], "uint16")
+        SCRATCH["h%s%d" % (_k, _n)] = ("sbuf", [128, K], "uint16")
+    for _k in ("t", "h", "g"):
+        SCRATCH["%s%d" % (_k, _n)] = ("sbuf", [128, 4 * C], "bfloat16")
+    SCRATCH["r%d" % _n] = ("sbuf", [128, 4 * C], "float32")
+    SCRATCH["z%d" % _n] = ("sbuf", [128, 4 * C], "bfloat16")
+    SCRATCH["zq%d" % _n] = ("sbuf", [128, C], "float8_e4m3fn_x4")
+    SCRATCH["zs%d" % _n] = ("sbuf", [128, C], "uint8")
+    SEMAPHORES += ["rq%d" % _n, "ra%d" % _n, "rk%d" % _n, "hq%d" % _n, "ha%d" % _n, "hk%d" % _n]
+
+
+def routes(topo, cores):
+    out = []
+    for d in STEP:
+        fl = {}
+        for r in range(N):
+            src, dst = cores[r], cores[(r + d) % N]
+            if topo.may_write(src, dst):
+                fl[r] = None
+                continue
+            near = [k for k in topo.cores_of(src) if k not in cores and topo.may_write(k, dst) and topo.die(k) == topo.die(src)]
+            far = [k for k in range(WORLD) if topo.mates(k, dst) and topo.may_write(src, k) and topo.may_write(k, dst)
+                   and topo.die(k) == topo.die(src)]
+            fl[r] = (near[0], near[-1], far[0])
+        out.append(fl)
+    return out
+
+
+def bits(m):
+    return bin(m).count("1")
+
+
+def hop_masks(topo, src, way):
+    far = topo.mask(src, way[2])
+    return [topo.mask(src, way[0]) & ~far, far]
+
+
+def rank_program(g, core, T, topo):
+    cores = list(T.cores)
+    ways = routes(topo, cores)
+    sent = [0]
+
+    def remote(dst, out, in_, sem):
+        rid, pid = topo.addr(dst, core)
+        m = topo.mask(core, dst)
+        g.remote_dma(out, in_, T.sem[sem], T.sem.ls, pid, rid, m)
+        sent[0] += bits(m)
+
+    def target(dst):
+        rid, pid = topo.addr(dst, core)
+        return DstId(rid=rid, pnc=pid)
+
+    def codes(name, a, b):
+        return T[name][:, a:b].bitcast(dt.uint8)
+
+    rank = T.rank_of(core)
+    if rank is None:
+        for n, d in enumerate(STEP):
+            for r in range(N):
+                if ways[n][r] is None:
+                    continue
+                src, dst = cores[r], cores[(r + d) % N]
+                near, lists, far = ways[n][r]
+                m = bits(topo.mask(src, core)) if core == lists else 0
+                if core in (near, far):
+                    m = bits(hop_masks(topo, src, ways[n][r])[0 if core == near else 1])
+                    a = 0 if core == near else H
+                    g.wait_ge(T.sem["hq%d" % n], 2 * m)
+                    remote(dst, codes("lq%d" % n, a, a + H), codes("hq%d" % n, 0, H), "rq%d" % n)
+                    remote(dst, T["lp%d" % n][:, a:a + H], T["hp%d" % n][:, 0:H], "rq%d" % n)
+                if core == lists:
+                    for k in "ak":
+                        g.wait_ge(T.sem["h%s%d" % (k, n)], m)
+                        remote(dst, T["l%s%d" % (k, n)][:], T["h%s%d" % (k, n)][:], "r%s%d" % (k, n))
+        if sent[0]:
+            g.wait_ge(T.sem.ls, sent[0])
+        return
+
+    queue = {"V": g.vector, "S": g.scalar, "P": g.tensor, "G": g, "Y": g.sync}
+    own = {"V": "sv", "S": "ss", "P": "sp", "G": "sg"}
+    count, hist, snap = {}, {}, {}
+    known = {q: {} for q in queue}
+    top = {}
+
+    def ap(v):
+        return T[v[0]][:, v[1]:v[2]] if v[3] == 1 else T[v[0]][:, v[1]:v[2]:v[3]]
+
+    def V(name, a=0, b=None, step=1):
+        return (name, a, T[name].shape[1] if b is None else b, step)
+
+    def new(name, n):
+        a = top.get(name, 0)
+        top[name] = a + n
+        assert a + n <= T[name].shape[1]
+        return (name, a, a + n, 1)
+
+    def sub(v, a, b):
+        return (v[0], v[1] + a, v[1] + b, 1)
+
+    def meet(u, v):
+        if u[2] <= v[1] or v[2] <= u[1]:
+            return False
+        return not (u[3] > 1 and u[3] == v[3] and (u[1] - v[1]) % u[3])
+
+    def note(tok, reads, writes, seen):
+        snap[tok] = dict(seen)
+        snap[tok][tok[0]] = max(tok[1], snap[tok].get(tok[0], 0))
+        for v in writes:
+            old = hist.setdefault(v[0], [])
+            hist[v[0]] = [h for h in old if not (v[3] == 1 and v[1] <= h[0][1] and h[0][2] <= v[2])] + [(v, tok, 1)]
+        for v in reads:
+            hist.setdefault(v[0], []).append((v, tok, 0))
+
+    def settle(q, reads, writes):
+        need = {}
+        for vs, both in ((reads, False), (writes, True)):
+            for v in vs:
+                for h, tok, w in hist.get(v[0], []):
+                    if (w or both) and meet(h, v) and known[q].get(tok[0], 0) < tok[1]:
+                        need[tok[0]] = max(need.get(tok[0], 0), tok[1])
+        toks = list(need.items())
+        for tok in toks:
+            if any(o != tok and snap[o].get(tok[0], 0) >= tok[1] for o in toks):
+                continue
+            queue[q].wait_ge(T.sem[tok[0]], tok[1])
+        for tok in toks:
+            for s, c in snap[tok].items():
+                known[q][s] = max(known[q].get(s, 0), c)
+
+    def op(q, call, reads, writes):
+        settle(q, reads, writes)
+        s = own[q]
+        count[s] = count.get(s, 0) + 1
+        call(queue[q]).then_inc(T.sem[s], 1)
+        note((s, count[s]), reads, writes, known[q])
+
+    def load(q, pairs, sem):
+        settle(q, [], [v for v, _ in pairs])
+        for v, src in pairs:
+            side = codes(v[0], v[1], v[2]) if v[0] == "wq" else ap(v)
+            queue[q].dma_start(side, src).then_inc(T.sem[sem], 16)
+            count[sem] = count.get(sem, 0) + 16
+        note((sem, count[sem]), [], [v for v, _ in pairs], known[q])
+
+    def store(q, pairs, sem):
+        settle(q, [v for _, v, _ in pairs], [])
+        for dst, v, side in pairs:
+            queue[q].dma_start(dst, side).then_inc(T.sem[sem], 16)
+            count[sem] = count.get(sem, 0) + 16
+
+    def tt(out, a, b, o):
+        op("V", lambda e: e.tensor_tensor(ap(out), ap(a), ap(b), o), [a, b], [out])
+
+    def ttg(out, win, lst, b, o):
+        op("V", lambda e: e.tensor_tensor(ap(out), ap(win).indirect(ap(lst)), ap(b), o), [win, lst, b], [out])
+
+    def ts(out, a, s1, o1, s2=None, o2=None):
+        cols = [s for s in (s1, s2) if isinstance(s, tuple)]
+        f = [ap(s) if isinstance(s, tuple) else s for s in (s1, s2)]
+        if o2 is None:
+            op("V", lambda e: e.tensor_scalar(ap(out), ap(a), f[0], None, o1), [a] + cols, [out])
+        else:
+            op("V", lambda e: e.tensor_scalar(ap(out), ap(a), f[0], f[1], o1, o2), [a] + cols, [out])
+
+    def cp(out, a):
+        op("V", lambda e: e.tensor_copy(ap(out), ap(a)), [a], [out])
+
+    def act(out, a, scale=1.0, bias=0.0):
+        op("S", lambda e: e.activation(ap(out), ap(a), COPY, bias=bias, scale=scale), [a], [out])
+
+    def pick(q, out, win, lst):
+        if q == "S":
+            op("S", lambda e: e.activation(ap(out), ap(win).indirect(ap(lst)), COPY), [win, lst], [out])
+        else:
+            op("V", lambda e: e.tensor_copy(ap(out), ap(win).indirect(ap(lst))), [win, lst], [out])
+
+    def scatter(win, lst, val):
+        op("V", lambda e: e.tensor_copy(ap(win).indirect(ap(lst)), ap(val)), [lst, val], [win])
+
+    def scan(out, d0, d1, init, o0, o1):
+        op("V", lambda e: e.tensor_tensor_scan(ap(out), ap(d0), ap(d1), init, o0, o1), [d0, d1], [out])
+
+    def quant(c, s, t):
+        op("V", lambda e: e.quantize_mx(out=ap(c), scales=ap(s), in_=ap(t)), [t], [c, s])
+
+    def mx(out, l, ls, r, rs):
+        op("P", lambda e: e.matmul_mx(ap(out), ap(l), ap(ls), ap(r), ap(rs), True, True), [l, ls, r, rs], [out])
+
+    R = lambda: new("rr", C)
+    B = lambda: new("rb", C)
+    off32, off16, pcf = V("off", 0, 1), V("off", 1, 2), V("off", 2, 3)
+    iof, c32 = V("io_f"), V("c32", 2 * C, 3 * C)
+    pc, pc15 = V("pc", 0, 1), V("pc", 1, 2)
+
+    def table(r, *outs):
+        sc = R()
+        scan(sc, c32, r, 0.0, A.add, A.max)
+        for o in outs:
+            ts(o, (sc[0], sc[1] + 15, sc[2], 16), off32, A.subtract)
+
+    load("Y", [(V("li", 0, K), T.cl[:]), (V("li", 2 * K, 3 * K), T.ml[:]), (V("li", K, 2 * K), T.pl[:])], "dl")
+    load("S", [(V("ut"), T.u[:])], "du")
+    load("Y", [(V("x0"), T.x[:])], "dx")
+    op("V", lambda e: e.memset(ap(V("eb")), 1.0), [], [V("eb")])
+    op("G", lambda e: e.iota(ap(V("dd")), [[1, C]], 128, -1), [], [V("dd")])
+    op("G", lambda e: e.iota(ap(pc), [[0, 1]], 0, 1), [], [pc])
+    op("G", lambda e: e.iota(ap(V("iw")), [[16, K]], 0, 0, allow_small_or_imprecise_dtypes=True), [], [V("iw")])
+    op("G", lambda e: e.iota(ap(iof), [[1, C]], 0, 0, allow_small_or_imprecise_dtypes=True), [], [iof])
+    for i in range(2):
+        v = V("kt", i * C, (i + 1) * C)
+        op("G", lambda e: e.iota(ap(v), [[512, C]], i * 2 ** 18, 0, allow_small_or_imprecise_dtypes=True), [], [v])
+        if i == 0:
+            op("G", lambda e: e.iota(ap(V("uo_i")), [[16, 8]], 0, 0), [], [V("uo_i")])
+            op("G", lambda e: e.affine_select(ap(V("eb")), ap(V("eb")), [[1, 520]], A.is_equal, 0.0, -4, -4), [V("eb")], [V("eb")])
+    ts(V("dd"), V("dd"), 15, A.bitwise_and)
+    ts(pc15, pc, 15, A.bitwise_and)
+    ts(V("c32", 0, C), V("dd"), 0.0, A.is_equal, -2.0 * BIG, A.mult)
+    ts(V("c32", C, 2 * C), V("dd"), 1.0, A.is_equal, BIG, A.mult)
+    cp(pcf, pc15)
+    ts(off32, pc15, 15.0, A.is_lt, BIG, A.mult)
+    ts(off16, pc15, 15.0, A.is_lt, BIGF, A.mult)
+    tt(c32, V("c32", 0, C), V("c32", C, 2 * C), A.add)
+    for i in range(2):
+        act(V("c16", i * C, i * C + C), c32, scale=2.0 ** -18)
+    lu = V("lu")
+    ib, bu = new("wf", 2 * K), new("wu", K)
+    ts(sub(ib, 0, K), V("iw"), pcf, A.add)
+    cp(lu, V("li"))
+    cu, au0, mu = sub(lu, 0, K), sub(lu, K, 2 * K), sub(lu, 2 * K, 3 * K)
+
+    Kc, bR, cR, cj = R(), R(), R(), new("wf", 2 * K)
+    ts(sub(cj, K, 2 * K), V("iw"), pcf, A.add)
+    cp(sub(cj, 0, K), V("li", 0, K))
+    pick("S", cR, iof, cu)
+    ttg(Kc, iof, cu, V("kt", 0, C), A.add)
+    scatter(bR, cu, iof)
+    table(bR, bu, sub(ib, K, 2 * K))
+
+    def links(ku):
+        ckR, GpR = R(), R()
+        pick("S", ckR, Kc, ku)
+        pick("S", GpR, ckR, bu)
+        return ckR, GpR
+
+    def ties(ckR):
+        ci, ck, gt, t, w, wf, wu = new("wi", K), new("wi", 2 * K), new("wf", 2 * K), new("wf", K), new("wf", K), new("wf", K), new("wu", K)
+        table(ckR, ci)
+        ts(sub(ck, 0, K), ci, 511, A.bitwise_and)
+        ts(sub(ck, K, 2 * K), ci, 9, A.arith_shift_right)
+        tt(gt, cj, ck, A.is_gt)
+        tt(t, sub(gt, 0, K), sub(gt, K, 2 * K), A.not_equal)
+        ts(w, t, float(C), A.mult)
+        tt(wf, w, sub(ck, 0, K), A.add)
+        cp(wu, wf)
+        return wu
+
+    def unlink(GpR):
+        gi, Gb, Gu = new("wi", K), new("wi", 2 * K), new("wu", K)
+        table(GpR, gi)
+        ts(sub(Gb, 0, K), gi, 511, A.bitwise_and)
+        ts(sub(Gb, K, 2 * K), gi, 9, A.arith_shift_right)
+        cp(Gu, sub(Gb, 0, K))
+        return Gb, Gu
+
+    def pairs(Gb):
+        l, lu = new("wf", 3 * K), new("wu", 4 * K)
+        g1, t2, dd = new("wf", 2 * K), new("wf", K), new("wf", 2 * K)
+        tt(sub(l, 0, 2 * K), ib, Gb, A.max)
+        tt(g1, ib, Gb, A.is_gt)
+        tt(sub(l, 2 * K, 3 * K), sub(ib, K, 2 * K), sub(Gb, K, 2 * K), A.min)
+        tt(t2, sub(g1, 0, K), sub(g1, K, 2 * K), A.not_equal)
+        cp(sub(lu, 0, 3 * K), l)
+        tt(dd, ib, Gb, A.subtract)
+        return lu, t2, dd
+
+    def cands(I):
+        q, gq, t, d, h, hu = [new("wi", 2 * K) for _ in range(3)] + [new("wf", 2 * K), new("wf", 2 * K), new("wu", 2 * K)]
+        ts(q, I, 511, A.bitwise_and)
+        ts(gq, I, 9, A.arith_shift_right, 511, A.bitwise_and)
+        tt(h, q, gq, A.max)
+        cp(hu, h)
+        ts(t, I, 18, A.arith_shift_right)
+        tt(d, q, gq, A.subtract)
+        return hu, gq, t, d
+
+    ckR, GpR = links(mu)
+    quant(V("uq"), V("us"), V("ut"))
+    cp(V("uo"), V("uo_i"))
+    op("V", lambda e: e.tensor_copy(T.pq[:, 0:128].bitcast(dt.uint32), T.uq[:, 0:128].bitcast(dt.uint32).indirect(T.uo[:, 0:8])),
+       [V("uq"), V("uo")], [V("pq")])
+    op("S", lambda e: e.activation(T.pl_s[:, 0:128], T.us[:, 0:128].indirect(T.uo[:, 0:8]), COPY), [V("us"), V("uo")], [V("pl_s")])
+    quant(V("q0"), V("s0"), V("x0"))
+    t1, tx, t3, t4, PQ, PQG = [R() for _ in range(6)]
+    ttg(t1, V("kt"), ties(ckR), cR, A.add)
+    scatter(tx, au0, t1)
+    Gb, Gu = unlink(GpR)
+    lists, t2, dd = pairs(Gb)
+    settle("Y", [V("x0")], [])
+    load("Y", [(V("wq"), T.wc[:]), (V("wp"), T.ws[:])], "dw")
+    load("Y", [(V("vt"), T.v[:])], "dv")
+    E4 = [V("eq", 128 * b, 128 * b + 128) for b in range(4)], [V("es", 128 * b, 128 * b + 128) for b in range(4)]
+    P4 = lambda name: [V(name, C * b, C * b + C) for b in range(4)]
+
+    for n, d in enumerate(STEP):
+        qn, sn = V("q%d" % n), V("s%d" % n)
+        dst, way = cores[(rank + d) % N], ways[n][rank]
+        gr = (rank - d) % N
+        gway, gsrc = ways[n][gr], cores[gr]
+        last = n == 2
+        settle("G", [qn, sn], [])
+        lists_to, kind = dst, "l"
+        if way is None:
+            remote(dst, codes("lq%d" % n, 0, C), codes(qn[0], 0, C), "rq%d" % n)
+            remote(dst, T["lp%d" % n][:], T[sn[0]][:], "rq%d" % n)
+        else:
+            m = hop_masks(topo, core, way)
+            for out, parts in ((codes("hq%d" % n, 0, H), [codes(qn[0], a, a + H) for a in (0, H)]),
+                               (T["hp%d" % n][:], [T[sn[0]][:, a:a + H] for a in (0, H)])):
+                g.remote_dma_fused([RemoteDMATransfer(dst_ids=[target(k)], dma_engine_mask=m[i], remote_sem=T.sem["hq%d" % n],
+                                                      srcs=[parts[i]], dsts=[out]) for i, k in ((1, way[2]), (0, way[0]))],
+                                   local_sem=T.sem.ls)
+                sent[0] += bits(m[0]) + bits(m[1])
+            lists_to, kind = way[1], "h"
+        if gway is None:
+            m = bits(topo.mask(gsrc, core))
+            arr = {"q": 2 * m, "a": m, "k": m}
+        else:
+            m = [bits(topo.mask(k, core)) for k in gway]
+            arr = {"q": 2 * (m[0] + m[2]), "a": m[1], "k": m[1]}
+        for k, vs in (("q", [V("lq%d" % n), V("lp%d" % n)]), ("a", [V("la%d" % n)]), ("k", [V("lk%d" % n)])):
+            note(("r%s%d" % (k, n), arr[k]), [], vs, {})
+
+        def send(k, v):
+            settle("G", [v], [])
+            remote(lists_to, T["%s%s%d" % (kind, k, n)][:], ap(v), "%s%s%d" % ("r" if kind == "l" else "h", k, n))
+
+        pz, pa = V("pz", 0, C), [V("pa", 512 * b, 512 * b + C) for b in range(4)]
+        tn, hn, gn, rn = [P4("%s%d" % (k, n)) for k in "thgr"]
+        mx(pz, V("pq"), V("pl_s"), qn, sn)
+        py = V("pz", 512, 512 + C)
+        mx(py, V("pq"), V("pl_s"), qn, sn)
+        SR, SV, h1 = R(), R(), R()
+        Ab, Bb, Bc, XN, fg, sc = [B() for _ in range(6)]
+        nq, sc2 = new("rb", 2 * C), new("rb", 2 * C)
+        I = new("wi", 2 * K)
+        if n:
+            table(PQ, sub(I, 0, K))
+            table(PQG, sub(I, K, 2 * K))
+            hu, gq, tq, dq = cands(I)
+        act(SR, pz)
+        cp(SV, py)
+        if n == 0:
+            pick("S", t3, tx, mu)
+            pick("S", t4, t3, au0)
+        pick("S", h1, SR, sub(lists, K, 2 * K))
+        ttg(Bb, SR, Gu, SV, A.is_ge)
+        if n:
+            for b in range(4):
+                mx(pa[b], E4[0][b], E4[1][b], qn, sn)
+            for b in range(2):
+                act(tn[b], pa[b])
+        act(Bc, Bb, bias=1.0)
+        if n == 0:
+            pick("S", PQ, t4, bu)
+            pick("S", PQG, PQ, Gu)
+        ttg(Ab, SR, sub(lists, 2 * K, 3 * K), h1, A.is_ge)
+        scan(XN, Ab, Bc, 1.0, A.min, A.add)
+        def far_flags():
+            pick("S", sub(nq, 0, C), XN, sub(hu, 0, K))
+            pick("S", sub(nq, C, 2 * C), XN, sub(hu, K, 2 * K))
+
+        if n == 0:
+            table(PQ, sub(I, 0, K))
+            table(PQG, sub(I, K, 2 * K))
+            hu, gq, tq, dq = cands(I)
+        far_flags()
+        if n:
+            for b in range(2, 4):
+                act(tn[b], pa[b])
+        pick("V", fg, XN, sub(lists, 0, K))
+        scan(sc, V("c16", 0, C), fg, 0.0, A.add, A.max)
+        nw, f2, sm, sa = new("wf", K), new("wf", 2 * K), new("wf", 2 * K), new("wf", 2 * K)
+        ts(nw, (sc[0], sc[1] + 15, sc[2], 16), off16, A.subtract, 2.0, A.not_equal)
+        tt(sub(f2, K, 2 * K), nw, t2, A.not_equal)
+        tt(sub(f2, 0, K), nw, t2, A.not_equal)
+        tt(sm, f2, dd, A.mult)
+        tt(sa, sm, Gb, A.add)
+        osa, ok = V("oa%d" % n), V("ok%d" % n)
+        su, oa = sub(osa, 0, K), sub(osa, K, 2 * K)
+        cp(osa, sa)
+        send("a", oa)
+        scan(sc2, V("c16"), nq, 0.0, A.add, A.max)
+        nqw, fq, km, k10 = [new("wf", 2 * K) for _ in range(4)]
+        ts(nqw, (sc2[0], sc2[1] + 15, sc2[2], 16), off16, A.subtract, 2.0, A.not_equal)
+        tt(fq, nqw, tq, A.not_equal)
+        tt(km, fq, dq, A.mult)
+        tt(k10, km, gq, A.add)
+        kd, ke, kf = [new("wf", K) for _ in range(3)]
+        tt(kd, sub(k10, 0, K), sub(k10, K, 2 * K), A.subtract)
+        tt(ke, kd, sub(f2, 0, K), A.mult)
+        tt(kf, ke, sub(k10, K, 2 * K), A.add)
+        cp(ok, kf)
+        send("k", ok)
+        if not last:
+            ckR, GpR = links(ok)
+        else:
+            pick("S", V("kr"), iof, ok)
+            store("Y", [(T.co[:, :], V("kr"), T.kr[0:128:16, :])], "dz")
+        if n == 0:
+            for b in range(4):
+                quant(E4[0][b], E4[1][b], V("eb", 4 - b, 516 - b))
+            for b in range(4):
+                mx(pa[b], E4[0][b], E4[1][b], qn, sn)
+        if not last:
+            t1, tx, t3, t4, PQ, PQG = [R() for _ in range(6)]
+            wu = ties(ckR)
+            Gb, Gu = unlink(GpR)
+        for b in range(4):
+            pb = V("pb", 512 * (b % 2), 512 * (b % 2) + C)
+            mx(pb, E4[0][b], E4[1][b], V("lq%d" % n), V("lp%d" % n))
+            if b == 3:
+                ts(hn[b], pb, 0.5, A.mult)
+            else:
+                act(hn[b], pb, scale=0.5)
+        if not last:
+            ttg(t1, V("kt"), wu, cR, A.add)
+        for b in range(4):
+            pick("S", gn[b], hn[b], V("la%d" % n))
+        for b in range(4):
+            ttg(V("z%d" % n, b, 4 * C, 4), hn[b], V("lk%d" % n), gn[b], A.add)
+        quant(V("zq%d" % n), V("zs%d" % n), V("z%d" % n))
+        if n == 0:
+            for b in range(4):
+                (act if b % 2 else cp)(tn[b], pa[b])
+        for b in range(4):
+            mx(pa[b], V("wq", 128 * b, 128 * b + 128), V("wp", 128 * b, 128 * b + 128), V("zq%d" % n), V("zs%d" % n))
+        if not last:
+            lists, t2, dd = pairs(Gb)
+            pick("S", tx, t1, su)
+            pick("S", t3, tx, Gu)
+        for b in range(4):
+            act(rn[b], pa[b], scale=0.03125)
+        if last:
+            quant(V("vq"), V("vs"), V("vt"))
+        if not last:
+            pick("S", t4, t3, su)
+            pick("S", PQ, t4, bu)
+            pick("S", PQG, PQ, Gu)
+        for b in range(4):
+            ttg(V("x%d" % (n + 1), b, 4 * C, 4), rn[b], oa, tn[b], A.add)
+        quant(V("q%d" % (n + 1)), V("s%d" % (n + 1)), V("x%d" % (n + 1)))
+
+    store("Y", [(T.oc[:, :], V("q3"), codes("q3", 0, C))], "dy")
+    store("S", [(T.osc[4 * k:4 * k + 4, :], V("s3"), T.s3[32 * k:32 * k + 4, 0:C]) for k in range(4)], "dy")
+    mx(V("pz", 0, C), V("vq"), V("vs"), V("q3"), V("s3"))
+    cp(V("yo", 0, H), V("pz", 0, H))
+    store("Y", [(T.y[:, 0:H], V("yo", 0, H), T.yo[:, 0:H])], "dy")
+    cp(V("yo", H, C), V("pz", H, C))
+    store("S", [(T.y[:, H:C], V("yo", H, C), T.yo[:, H:C])], "dy")
+    for s in sorted(count):
+        if known["G"].get(s, 0) < count[s]:
+            g.wait_ge(T.sem[s], count[s])
+    g.wait_ge(T.sem.ls, sent[0])

@@ -14,7 +14,7 @@ COPY = ActivationFunctionType.Copy
 SCRATCH = {
     "li": ("sbuf", [128, 3 * K], "int32"), "lu": ("sbuf", [128, 3 * K], "uint16"),
     "pc": ("sbuf", [128, 2], "int32"), "off": ("sbuf", [128, 4], "float32"), "iw": ("sbuf", [128, K], "float32"),
-    "dd": ("sbuf", [128, C], "int32"), "c32": ("sbuf", [128, 3 * C], "float32"), "c16": ("sbuf", [128, 2 * C], "bfloat16"),
+    "dd": ("sbuf", [128, C], "float32"), "sg": ("sbuf", [128, C], "float32"), "c32": ("sbuf", [128, C], "float32"), "c16": ("sbuf", [128, 2 * C], "bfloat16"),
     "io_f": ("sbuf", [128, C], "float32"), "kt": ("sbuf", [128, 2 * C], "float32"),
     "rr": ("sbuf", [128, 60 * C], "float32"), "rb": ("sbuf", [128, 30 * C], "bfloat16"),
     "wf": ("sbuf", [128, 150 * K], "float32"), "wi": ("sbuf", [128, 50 * K], "int32"), "wu": ("sbuf", [128, 40 * K], "uint16"),
@@ -41,40 +41,53 @@ for _n in range(3):
     for _k in "ak":
         SCRATCH["o%s%d" % (_k, _n)] = ("sbuf", [128, 2 * K if _k == "a" else K], "uint16")
         SCRATCH["l%s%d" % (_k, _n)] = ("sbuf", [128, K], "uint16")
-        SCRATCH["h%s%d" % (_k, _n)] = ("sbuf", [128, K], "uint16")
+        for _i in range(2):
+            SCRATCH["h%s%d%d" % (_k, _n, _i)] = ("sbuf", [128, K], "uint16")
+            SEMAPHORES += ["h%s%d%d" % (_k, _n, _i)]
     for _k in ("t", "h", "g"):
         SCRATCH["%s%d" % (_k, _n)] = ("sbuf", [128, 4 * C], "bfloat16")
     SCRATCH["r%d" % _n] = ("sbuf", [128, 4 * C], "float32")
     SCRATCH["z%d" % _n] = ("sbuf", [128, 4 * C], "bfloat16")
     SCRATCH["zq%d" % _n] = ("sbuf", [128, C], "float8_e4m3fn_x4")
     SCRATCH["zs%d" % _n] = ("sbuf", [128, C], "uint8")
-    SEMAPHORES += ["rq%d" % _n, "ra%d" % _n, "rk%d" % _n, "hq%d" % _n, "ha%d" % _n, "hk%d" % _n]
+    SEMAPHORES += ["rq%d" % _n, "ra%d" % _n, "rk%d" % _n, "hq%d" % _n, "hp%d" % _n]
 
 
 def routes(topo, cores):
-    out = []
+    out, desk = [], {}
     for d in STEP:
-        fl = {}
-        for r in range(N):
-            src, dst = cores[r], cores[(r + d) % N]
-            if topo.may_write(src, dst):
-                fl[r] = None
-                continue
-            near = [k for k in topo.cores_of(src) if k not in cores and topo.may_write(k, dst) and topo.die(k) == topo.die(src)]
-            far = [k for k in range(WORLD) if topo.mates(k, dst) and topo.may_write(src, k) and topo.may_write(k, dst)
-                   and topo.die(k) == topo.die(src)]
-            fl[r] = (near[0], near[-1], far[0])
+        ends = [(cores[r], cores[(r + d) % N]) for r in range(N)]
+        cross = [r for r in range(N) if not topo.may_write(*ends[r])]
+        fl, taken = [None] * N, {}
+        for r in reversed(cross):
+            src, dst = ends[r]
+            chip = topo.cores_of(src)
+            alone = sum(ends[s][0] in chip for s in cross) == 1
+            near, far = [], []
+            for e in sorted({topo.die(k) for k in chip}, key=lambda e: e != topo.die(src))[:2 if alone else 1]:
+                port = [k for k in chip if k not in cores and topo.may_write(k, dst) and topo.die(k) == e]
+                near.append(port[0])
+                if len(near) == 1:
+                    desk.setdefault(chip[0], port[-1])
+                far.append([k for k in range(WORLD) if topo.mates(k, dst) and topo.may_write(src, k) and topo.may_write(k, dst)
+                            and topo.die(k) == e][0])
+            out_e = topo.engines(src, far[0])
+            in_e = [e for e in topo.engines(src, near[0]) if e not in out_e]
+            w, parts = C // (2 * len(near)), []
+            for cs, es in ((far, out_e), (near, in_e)):
+                for i, k in enumerate(cs):
+                    z = len(es) // len(cs)
+                    a = w * len(parts)
+                    parts.append((k, a, a + w, sum(1 << e for e in es[z * i:z * i + z])))
+            k = desk[chip[0]]
+            fl[r] = parts, (k, taken.get(k, 0))
+            taken[k] = taken.get(k, 0) + 1
         out.append(fl)
     return out
 
 
 def bits(m):
     return bin(m).count("1")
-
-
-def hop_masks(topo, src, way):
-    far = topo.mask(src, way[2])
-    return [topo.mask(src, way[0]) & ~far, far]
 
 
 def rank_program(g, core, T, topo):
@@ -98,22 +111,22 @@ def rank_program(g, core, T, topo):
     rank = T.rank_of(core)
     if rank is None:
         for n, d in enumerate(STEP):
-            for r in range(N):
+            for r in reversed(range(N)):
                 if ways[n][r] is None:
                     continue
                 src, dst = cores[r], cores[(r + d) % N]
-                near, lists, far = ways[n][r]
-                m = bits(topo.mask(src, core)) if core == lists else 0
-                if core in (near, far):
-                    m = bits(hop_masks(topo, src, ways[n][r])[0 if core == near else 1])
-                    a = 0 if core == near else H
-                    g.wait_ge(T.sem["hq%d" % n], 2 * m)
-                    remote(dst, codes("lq%d" % n, a, a + H), codes("hq%d" % n, 0, H), "rq%d" % n)
-                    remote(dst, T["lp%d" % n][:, a:a + H], T["hp%d" % n][:, 0:H], "rq%d" % n)
-                if core == lists:
+                parts, (desk, slot) = ways[n][r]
+                for k, a, b, m in parts:
+                    if core == k:
+                        g.wait_ge(T.sem["hq%d" % n], bits(m))
+                        remote(dst, codes("lq%d" % n, a, b), codes("hq%d" % n, 0, b - a), "rq%d" % n)
+                        g.wait_ge(T.sem["hp%d" % n], bits(m))
+                        remote(dst, T["lp%d" % n][:, a:b], T["hp%d" % n][:, 0:b - a], "rq%d" % n)
+                if core == desk:
                     for k in "ak":
-                        g.wait_ge(T.sem["h%s%d" % (k, n)], m)
-                        remote(dst, T["l%s%d" % (k, n)][:], T["h%s%d" % (k, n)][:], "r%s%d" % (k, n))
+                        h = "h%s%d%d" % (k, n, slot)
+                        g.wait_ge(T.sem[h], bits(topo.mask(src, core)))
+                        remote(dst, T["l%s%d" % (k, n)][:], T[h][:], "r%s%d" % (k, n))
         if sent[0]:
             g.wait_ge(T.sem.ls, sent[0])
         return
@@ -230,8 +243,8 @@ def rank_program(g, core, T, topo):
 
     R = lambda: new("rr", C)
     B = lambda: new("rb", C)
-    off32, off16, pcf = V("off", 0, 1), V("off", 1, 2), V("off", 2, 3)
-    iof, c32 = V("io_f"), V("c32", 2 * C, 3 * C)
+    off32, off16, pcf, half = V("off", 0, 1), V("off", 1, 2), V("off", 2, 3), V("off", 3, 4)
+    iof, c32 = V("io_f"), V("c32")
     pc, pc15 = V("pc", 0, 1), V("pc", 1, 2)
 
     def table(r, *outs):
@@ -244,26 +257,26 @@ def rank_program(g, core, T, topo):
     load("S", [(V("ut"), T.u[:])], "du")
     load("Y", [(V("x0"), T.x[:])], "dx")
     op("V", lambda e: e.memset(ap(V("eb")), 1.0), [], [V("eb")])
-    op("G", lambda e: e.iota(ap(V("dd")), [[1, C]], 128, -1), [], [V("dd")])
     op("G", lambda e: e.iota(ap(pc), [[0, 1]], 0, 1), [], [pc])
+    op("G", lambda e: e.iota(ap(V("dd")), [[0, K], [1, 16]], 0, 0, allow_small_or_imprecise_dtypes=True), [], [V("dd")])
+    op("G", lambda e: e.iota(ap(V("uo_i")), [[16, 8]], 0, 0), [], [V("uo_i")])
     op("G", lambda e: e.iota(ap(V("iw")), [[16, K]], 0, 0, allow_small_or_imprecise_dtypes=True), [], [V("iw")])
     op("G", lambda e: e.iota(ap(iof), [[1, C]], 0, 0, allow_small_or_imprecise_dtypes=True), [], [iof])
     for i in range(2):
         v = V("kt", i * C, (i + 1) * C)
         op("G", lambda e: e.iota(ap(v), [[512, C]], i * 2 ** 18, 0, allow_small_or_imprecise_dtypes=True), [], [v])
         if i == 0:
-            op("G", lambda e: e.iota(ap(V("uo_i")), [[16, 8]], 0, 0), [], [V("uo_i")])
             op("G", lambda e: e.affine_select(ap(V("eb")), ap(V("eb")), [[1, 520]], A.is_equal, 0.0, -4, -4), [V("eb")], [V("eb")])
-    ts(V("dd"), V("dd"), 15, A.bitwise_and)
     ts(pc15, pc, 15, A.bitwise_and)
-    ts(V("c32", 0, C), V("dd"), 0.0, A.is_equal, -2.0 * BIG, A.mult)
-    ts(V("c32", C, 2 * C), V("dd"), 1.0, A.is_equal, BIG, A.mult)
+    ts(half, pc15, -1.0, A.mult, -0.5, A.add)
     cp(pcf, pc15)
-    ts(off32, pc15, 15.0, A.is_lt, BIG, A.mult)
-    ts(off16, pc15, 15.0, A.is_lt, BIGF, A.mult)
-    tt(c32, V("c32", 0, C), V("c32", C, 2 * C), A.add)
+    op("S", lambda e: e.activation(ap(V("sg")), ap(V("dd")), ActivationFunctionType.Sign, bias=ap(half)), [V("dd"), half], [V("sg")])
+    ts(off32, pc15, -BIG, A.mult, 15.0 * BIG, A.add)
+    ts(off16, pc15, -BIGF, A.mult, 15.0 * BIGF, A.add)
+    ts(c32, V("sg"), 8.5 * BIG, A.mult, -7.5 * BIG, A.add)
     for i in range(2):
-        act(V("c16", i * C, i * C + C), c32, scale=2.0 ** -18)
+        act(V("c16", i * C, i * C + C), V("sg"), scale=9.0 * BIGF, bias=-8.0 * BIGF)
+    cp(V("uo"), V("uo_i"))
     lu = V("lu")
     ib, bu = new("wf", 2 * K), new("wu", K)
     ts(sub(ib, 0, K), V("iw"), pcf, A.add)
@@ -284,58 +297,55 @@ def rank_program(g, core, T, topo):
         pick("S", GpR, ckR, bu)
         return ckR, GpR
 
-    def ties(ckR):
+    def ties(ckR, GpR):
         ci, ck, gt, t, w, wf, wu = new("wi", K), new("wi", 2 * K), new("wf", 2 * K), new("wf", K), new("wf", K), new("wf", K), new("wu", K)
+        gi, Gb, Gu, sc = new("wi", K), new("wi", 2 * K), new("wu", K), R()
         table(ckR, ci)
         ts(sub(ck, 0, K), ci, 511, A.bitwise_and)
         ts(sub(ck, K, 2 * K), ci, 9, A.arith_shift_right)
+        scan(sc, c32, GpR, 0.0, A.add, A.max)
         tt(gt, cj, ck, A.is_gt)
+        ts(gi, (sc[0], sc[1] + 15, sc[2], 16), off32, A.subtract)
         tt(t, sub(gt, 0, K), sub(gt, K, 2 * K), A.not_equal)
-        ts(w, t, float(C), A.mult)
-        tt(wf, w, sub(ck, 0, K), A.add)
-        cp(wu, wf)
-        return wu
-
-    def unlink(GpR):
-        gi, Gb, Gu = new("wi", K), new("wi", 2 * K), new("wu", K)
-        table(GpR, gi)
         ts(sub(Gb, 0, K), gi, 511, A.bitwise_and)
+        ts(w, t, float(C), A.mult)
         ts(sub(Gb, K, 2 * K), gi, 9, A.arith_shift_right)
+        tt(wf, w, sub(ck, 0, K), A.add)
         cp(Gu, sub(Gb, 0, K))
-        return Gb, Gu
+        cp(wu, wf)
+        return wu, Gb, Gu
 
     def pairs(Gb):
         l, lu = new("wf", 3 * K), new("wu", 4 * K)
         g1, t2, dd = new("wf", 2 * K), new("wf", K), new("wf", 2 * K)
         tt(sub(l, 0, 2 * K), ib, Gb, A.max)
-        tt(g1, ib, Gb, A.is_gt)
         tt(sub(l, 2 * K, 3 * K), sub(ib, K, 2 * K), sub(Gb, K, 2 * K), A.min)
-        tt(t2, sub(g1, 0, K), sub(g1, K, 2 * K), A.not_equal)
+        tt(g1, ib, Gb, A.is_gt)
         cp(sub(lu, 0, 3 * K), l)
         tt(dd, ib, Gb, A.subtract)
+        tt(t2, sub(g1, 0, K), sub(g1, K, 2 * K), A.not_equal)
         return lu, t2, dd
 
     def cands(I):
         q, gq, t, d, h, hu = [new("wi", 2 * K) for _ in range(3)] + [new("wf", 2 * K), new("wf", 2 * K), new("wu", 2 * K)]
         ts(q, I, 511, A.bitwise_and)
         ts(gq, I, 9, A.arith_shift_right, 511, A.bitwise_and)
-        tt(h, q, gq, A.max)
-        cp(hu, h)
         ts(t, I, 18, A.arith_shift_right)
+        tt(h, q, gq, A.max)
         tt(d, q, gq, A.subtract)
+        cp(hu, h)
         return hu, gq, t, d
 
     ckR, GpR = links(mu)
     quant(V("uq"), V("us"), V("ut"))
-    cp(V("uo"), V("uo_i"))
+    op("S", lambda e: e.activation(T.pl_s[:, 0:128], T.us[:, 0:128].indirect(T.uo[:, 0:8]), COPY), [V("us"), V("uo")], [V("pl_s")])
     op("V", lambda e: e.tensor_copy(T.pq[:, 0:128].bitcast(dt.uint32), T.uq[:, 0:128].bitcast(dt.uint32).indirect(T.uo[:, 0:8])),
        [V("uq"), V("uo")], [V("pq")])
-    op("S", lambda e: e.activation(T.pl_s[:, 0:128], T.us[:, 0:128].indirect(T.uo[:, 0:8]), COPY), [V("us"), V("uo")], [V("pl_s")])
     quant(V("q0"), V("s0"), V("x0"))
     t1, tx, t3, t4, PQ, PQG = [R() for _ in range(6)]
-    ttg(t1, V("kt"), ties(ckR), cR, A.add)
+    wu, Gb, Gu = ties(ckR, GpR)
+    ttg(t1, V("kt"), wu, cR, A.add)
     scatter(tx, au0, t1)
-    Gb, Gu = unlink(GpR)
     lists, t2, dd = pairs(Gb)
     settle("Y", [V("x0")], [])
     load("Y", [(V("wq"), T.wc[:]), (V("wp"), T.ws[:])], "dw")
@@ -350,31 +360,32 @@ def rank_program(g, core, T, topo):
         gway, gsrc = ways[n][gr], cores[gr]
         last = n == 2
         settle("G", [qn, sn], [])
-        lists_to, kind = dst, "l"
         if way is None:
             remote(dst, codes("lq%d" % n, 0, C), codes(qn[0], 0, C), "rq%d" % n)
             remote(dst, T["lp%d" % n][:], T[sn[0]][:], "rq%d" % n)
         else:
-            m = hop_masks(topo, core, way)
-            for out, parts in ((codes("hq%d" % n, 0, H), [codes(qn[0], a, a + H) for a in (0, H)]),
-                               (T["hp%d" % n][:], [T[sn[0]][:, a:a + H] for a in (0, H)])):
-                g.remote_dma_fused([RemoteDMATransfer(dst_ids=[target(k)], dma_engine_mask=m[i], remote_sem=T.sem["hq%d" % n],
-                                                      srcs=[parts[i]], dsts=[out]) for i, k in ((1, way[2]), (0, way[0]))],
+            for kind, piece in (("hq%d" % n, lambda a, b: (codes("hq%d" % n, 0, b - a), codes(qn[0], a, b))),
+                                ("hp%d" % n, lambda a, b: (T["hp%d" % n][:, 0:b - a], T[sn[0]][:, a:b]))):
+                g.remote_dma_fused([RemoteDMATransfer(dst_ids=[target(k)], dma_engine_mask=m, remote_sem=T.sem[kind],
+                                                      srcs=[piece(a, b)[1]], dsts=[piece(a, b)[0]]) for k, a, b, m in way[0]],
                                    local_sem=T.sem.ls)
-                sent[0] += bits(m[0]) + bits(m[1])
-            lists_to, kind = way[1], "h"
+                sent[0] += sum(bits(m) for _, _, _, m in way[0])
         if gway is None:
             m = bits(topo.mask(gsrc, core))
             arr = {"q": 2 * m, "a": m, "k": m}
         else:
-            m = [bits(topo.mask(k, core)) for k in gway]
-            arr = {"q": 2 * (m[0] + m[2]), "a": m[1], "k": m[1]}
+            m = bits(topo.mask(gway[1][0], core))
+            arr = {"q": 2 * sum(bits(topo.mask(p[0], core)) for p in gway[0]), "a": m, "k": m}
         for k, vs in (("q", [V("lq%d" % n), V("lp%d" % n)]), ("a", [V("la%d" % n)]), ("k", [V("lk%d" % n)])):
             note(("r%s%d" % (k, n), arr[k]), [], vs, {})
 
         def send(k, v):
             settle("G", [v], [])
-            remote(lists_to, T["%s%s%d" % (kind, k, n)][:], ap(v), "%s%s%d" % ("r" if kind == "l" else "h", k, n))
+            if way is None:
+                remote(dst, T["l%s%d" % (k, n)][:], ap(v), "r%s%d" % (k, n))
+            else:
+                h = "h%s%d%d" % (k, n, way[1][1])
+                remote(way[1][0], T[h][:], ap(v), h)
 
         pz, pa = V("pz", 0, C), [V("pa", 512 * b, 512 * b + C) for b in range(4)]
         tn, hn, gn, rn = [P4("%s%d" % (k, n)) for k in "thgr"]
@@ -385,16 +396,23 @@ def rank_program(g, core, T, topo):
         Ab, Bb, Bc, XN, fg, sc = [B() for _ in range(6)]
         nq, sc2 = new("rb", 2 * C), new("rb", 2 * C)
         I = new("wi", 2 * K)
+        sq = new("rr", 2 * C)
+
+        def targets():
+            scan(sub(sq, 0, C), c32, PQ, 0.0, A.add, A.max)
+            scan(sub(sq, C, 2 * C), c32, PQG, 0.0, A.add, A.max)
+            ts(I, (sq[0], sq[1] + 15, sq[2], 16), off32, A.subtract)
+            return cands(I)
+
         if n:
-            table(PQ, sub(I, 0, K))
-            table(PQG, sub(I, K, 2 * K))
-            hu, gq, tq, dq = cands(I)
+            hu, gq, tq, dq = targets()
         act(SR, pz)
         cp(SV, py)
         if n == 0:
             pick("S", t3, tx, mu)
-            pick("S", t4, t3, au0)
         pick("S", h1, SR, sub(lists, K, 2 * K))
+        if n == 0:
+            pick("S", t4, t3, au0)
         ttg(Bb, SR, Gu, SV, A.is_ge)
         if n:
             for b in range(4):
@@ -412,35 +430,39 @@ def rank_program(g, core, T, topo):
             pick("S", sub(nq, C, 2 * C), XN, sub(hu, K, 2 * K))
 
         if n == 0:
-            table(PQ, sub(I, 0, K))
-            table(PQG, sub(I, K, 2 * K))
-            hu, gq, tq, dq = cands(I)
+            for b in range(4):
+                quant(E4[0][b], E4[1][b], V("eb", 4 - b, 516 - b))
+            for b in range(4):
+                mx(pa[b], E4[0][b], E4[1][b], qn, sn)
+            hu, gq, tq, dq = targets()
         far_flags()
-        if n:
-            for b in range(2, 4):
-                act(tn[b], pa[b])
+        for b in (2, 3) if n else (0, 1):
+            act(tn[b], pa[b])
         pick("V", fg, XN, sub(lists, 0, K))
         scan(sc, V("c16", 0, C), fg, 0.0, A.add, A.max)
-        nw, f2, sm, sa = new("wf", K), new("wf", 2 * K), new("wf", 2 * K), new("wf", 2 * K)
+        nw, f3, sm, sa = new("wf", K), new("wf", 3 * K), new("wf", 2 * K), new("wf", 2 * K)
+        Pm, Pe, P0 = new("wf", 2 * K), new("wf", 2 * K), new("wf", K)
         ts(nw, (sc[0], sc[1] + 15, sc[2], 16), off16, A.subtract, 2.0, A.not_equal)
-        tt(sub(f2, K, 2 * K), nw, t2, A.not_equal)
-        tt(sub(f2, 0, K), nw, t2, A.not_equal)
-        tt(sm, f2, dd, A.mult)
+        tt(sub(f3, 0, K), nw, t2, A.not_equal)
+        tt(sub(f3, K, 2 * K), nw, t2, A.not_equal)
+        tt(sub(f3, 2 * K, 3 * K), nw, t2, A.is_equal)
+        tt(sm, sub(f3, 0, 2 * K), dd, A.mult)
+        tt(Pe, sub(f3, K, 3 * K), gq, A.mult)
         tt(sa, sm, Gb, A.add)
+        tt(Pm, sub(f3, K, 3 * K), dq, A.mult)
         osa, ok = V("oa%d" % n), V("ok%d" % n)
         su, oa = sub(osa, 0, K), sub(osa, K, 2 * K)
         cp(osa, sa)
         send("a", oa)
+        tt(P0, sub(Pe, 0, K), sub(Pe, K, 2 * K), A.add)
         scan(sc2, V("c16"), nq, 0.0, A.add, A.max)
-        nqw, fq, km, k10 = [new("wf", 2 * K) for _ in range(4)]
+        nqw, fq, km = [new("wf", 2 * K) for _ in range(3)]
         ts(nqw, (sc2[0], sc2[1] + 15, sc2[2], 16), off16, A.subtract, 2.0, A.not_equal)
         tt(fq, nqw, tq, A.not_equal)
-        tt(km, fq, dq, A.mult)
-        tt(k10, km, gq, A.add)
-        kd, ke, kf = [new("wf", K) for _ in range(3)]
-        tt(kd, sub(k10, 0, K), sub(k10, K, 2 * K), A.subtract)
-        tt(ke, kd, sub(f2, 0, K), A.mult)
-        tt(kf, ke, sub(k10, K, 2 * K), A.add)
+        tt(km, fq, Pm, A.mult)
+        ke, kf = new("wf", K), new("wf", K)
+        tt(ke, sub(km, 0, K), sub(km, K, 2 * K), A.add)
+        tt(kf, ke, P0, A.add)
         cp(ok, kf)
         send("k", ok)
         if not last:
@@ -448,15 +470,9 @@ def rank_program(g, core, T, topo):
         else:
             pick("S", V("kr"), iof, ok)
             store("Y", [(T.co[:, :], V("kr"), T.kr[0:128:16, :])], "dz")
-        if n == 0:
-            for b in range(4):
-                quant(E4[0][b], E4[1][b], V("eb", 4 - b, 516 - b))
-            for b in range(4):
-                mx(pa[b], E4[0][b], E4[1][b], qn, sn)
         if not last:
             t1, tx, t3, t4, PQ, PQG = [R() for _ in range(6)]
-            wu = ties(ckR)
-            Gb, Gu = unlink(GpR)
+            wu, Gb, Gu = ties(ckR, GpR)
         for b in range(4):
             pb = V("pb", 512 * (b % 2), 512 * (b % 2) + C)
             mx(pb, E4[0][b], E4[1][b], V("lq%d" % n), V("lp%d" % n))
@@ -472,8 +488,8 @@ def rank_program(g, core, T, topo):
             ttg(V("z%d" % n, b, 4 * C, 4), hn[b], V("lk%d" % n), gn[b], A.add)
         quant(V("zq%d" % n), V("zs%d" % n), V("z%d" % n))
         if n == 0:
-            for b in range(4):
-                (act if b % 2 else cp)(tn[b], pa[b])
+            for b in (2, 3):
+                cp(tn[b], pa[b])
         for b in range(4):
             mx(pa[b], V("wq", 128 * b, 128 * b + 128), V("wp", 128 * b, 128 * b + 128), V("zq%d" % n), V("zs%d" % n))
         if not last:

@@ -26,7 +26,7 @@ SCRATCH = {
     "vt": ("sbuf", [128, 512], "bfloat16"), "vq": ("sbuf", [128, 128], "float8_e4m3fn_x4"), "vs": ("sbuf", [128, 128], "uint8"),
     "wq": ("sbuf", [128, 512], "float8_e4m3fn_x4"), "wp": ("sbuf", [128, 512], "uint8"),
     "yo": ("sbuf", [128, C], "float32"),
-    "pa": ("psum", [128, 2048], "float32"), "pb": ("psum", [128, 1024], "float32"), "pz": ("psum", [128, 1024], "float32"),
+    "pa": ("psum", [128, 2048], "float32"), "pb": ("psum", [128, 1536], "float32"), "pz": ("psum", [128, 512], "float32"),
 }
 SEMAPHORES = ["sv", "ss", "sp", "sg", "dl", "du", "dx", "dw", "dv", "dy", "dz", "ls"]
 for _n in range(4):
@@ -316,24 +316,23 @@ def rank_program(g, core, T, topo):
         return wu, Gb, Gu
 
     def pairs(Gb):
-        l, lu = new("wf", 3 * K), new("wu", 4 * K)
+        l, lu = new("wf", 4 * K), new("wu", 4 * K)
         g1, t2, dd = new("wf", 2 * K), new("wf", K), new("wf", 2 * K)
         tt(sub(l, 0, 2 * K), ib, Gb, A.max)
-        tt(sub(l, 2 * K, 3 * K), sub(ib, K, 2 * K), sub(Gb, K, 2 * K), A.min)
+        tt(sub(l, 2 * K, 4 * K), ib, Gb, A.min)
         tt(g1, ib, Gb, A.is_gt)
-        cp(sub(lu, 0, 3 * K), l)
+        cp(lu, l)
         tt(dd, ib, Gb, A.subtract)
         tt(t2, sub(g1, 0, K), sub(g1, K, 2 * K), A.not_equal)
         return lu, t2, dd
 
     def cands(I):
-        q, gq, t, d, h, hu = [new("wi", 2 * K) for _ in range(3)] + [new("wf", 2 * K), new("wf", 2 * K), new("wu", 2 * K)]
+        q, gq, t, d, hu = [new("wi", 2 * K) for _ in range(3)] + [new("wf", 2 * K), new("wu", 2 * K)]
         ts(q, I, 511, A.bitwise_and)
         ts(gq, I, 9, A.arith_shift_right, 511, A.bitwise_and)
+        cp(hu, q)
         ts(t, I, 18, A.arith_shift_right)
-        tt(h, q, gq, A.max)
         tt(d, q, gq, A.subtract)
-        cp(hu, h)
         return hu, gq, t, d
 
     ckR, GpR = links(mu)
@@ -345,8 +344,8 @@ def rank_program(g, core, T, topo):
     t1, tx, t3, t4, PQ, PQG = [R() for _ in range(6)]
     wu, Gb, Gu = ties(ckR, GpR)
     ttg(t1, V("kt"), wu, cR, A.add)
-    scatter(tx, au0, t1)
     lists, t2, dd = pairs(Gb)
+    scatter(tx, au0, t1)
     settle("Y", [V("x0")], [])
     load("Y", [(V("wq"), T.wc[:]), (V("wp"), T.ws[:])], "dw")
     load("Y", [(V("vt"), T.v[:])], "dv")
@@ -390,10 +389,8 @@ def rank_program(g, core, T, topo):
         pz, pa = V("pz", 0, C), [V("pa", 512 * b, 512 * b + C) for b in range(4)]
         tn, hn, gn, rn = [P4("%s%d" % (k, n)) for k in "thgr"]
         mx(pz, V("pq"), V("pl_s"), qn, sn)
-        py = V("pz", 512, 512 + C)
-        mx(py, V("pq"), V("pl_s"), qn, sn)
-        SR, SV, h1 = R(), R(), R()
-        Ab, Bb, Bc, XN, fg, sc = [B() for _ in range(6)]
+        SR, h1, h2 = R(), R(), R()
+        Ab, Bb, Bc, XN, sc = [B() for _ in range(5)]
         nq, sc2 = new("rb", 2 * C), new("rb", 2 * C)
         I = new("wi", 2 * K)
         sq = new("rr", 2 * C)
@@ -407,59 +404,57 @@ def rank_program(g, core, T, topo):
         if n:
             hu, gq, tq, dq = targets()
         act(SR, pz)
-        cp(SV, py)
+        pick("S", h2, SR, sub(lists, 0, K))
+        pick("S", h1, SR, sub(lists, K, 2 * K))
+        ttg(Bb, SR, sub(lists, 2 * K, 3 * K), h2, A.is_ge)
         if n == 0:
             pick("S", t3, tx, mu)
-        pick("S", h1, SR, sub(lists, K, 2 * K))
-        if n == 0:
-            pick("S", t4, t3, au0)
-        ttg(Bb, SR, Gu, SV, A.is_ge)
         if n:
-            for b in range(4):
-                mx(pa[b], E4[0][b], E4[1][b], qn, sn)
-            for b in range(2):
-                act(tn[b], pa[b])
-        act(Bc, Bb, bias=1.0)
-        if n == 0:
+            act(Bc, Bb, bias=1.0)
+        else:
+            ts(Bc, Bb, 1.0, A.add)
+            pick("S", t4, t3, au0)
             pick("S", PQ, t4, bu)
             pick("S", PQG, PQ, Gu)
-        ttg(Ab, SR, sub(lists, 2 * K, 3 * K), h1, A.is_ge)
+        ttg(Ab, SR, sub(lists, 3 * K, 4 * K), h1, A.is_ge)
         scan(XN, Ab, Bc, 1.0, A.min, A.add)
-        def far_flags():
-            pick("S", sub(nq, 0, C), XN, sub(hu, 0, K))
-            pick("S", sub(nq, C, 2 * C), XN, sub(hu, K, 2 * K))
-
         if n == 0:
             for b in range(4):
                 quant(E4[0][b], E4[1][b], V("eb", 4 - b, 516 - b))
-            for b in range(4):
-                mx(pa[b], E4[0][b], E4[1][b], qn, sn)
+        for b in range(4):
+            mx(pa[b], E4[0][b], E4[1][b], qn, sn)
+        if n == 0:
             hu, gq, tq, dq = targets()
-        far_flags()
-        for b in (2, 3) if n else (0, 1):
+        pick("S", sub(nq, 0, C), XN, sub(hu, 0, K))
+        pick("S", sub(nq, C, 2 * C), XN, sub(hu, K, 2 * K))
+        for b in range(2):
             act(tn[b], pa[b])
-        pick("V", fg, XN, sub(lists, 0, K))
-        scan(sc, V("c16", 0, C), fg, 0.0, A.add, A.max)
+        scan(sc, V("c16", 0, C), XN, 0.0, A.add, A.max)
         nw, f3, sm, sa = new("wf", K), new("wf", 3 * K), new("wf", 2 * K), new("wf", 2 * K)
         Pm, Pe, P0 = new("wf", 2 * K), new("wf", 2 * K), new("wf", K)
+        s2, qt, qd, qe = [new("wf", 2 * K) for _ in range(4)]
         ts(nw, (sc[0], sc[1] + 15, sc[2], 16), off16, A.subtract, 2.0, A.not_equal)
+        ts(s2, tq, -2.0, A.mult, 1.0, A.add)
         tt(sub(f3, 0, K), nw, t2, A.not_equal)
         tt(sub(f3, K, 2 * K), nw, t2, A.not_equal)
-        tt(sub(f3, 2 * K, 3 * K), nw, t2, A.is_equal)
+        tt(qt, tq, dq, A.mult)
         tt(sm, sub(f3, 0, 2 * K), dd, A.mult)
-        tt(Pe, sub(f3, K, 3 * K), gq, A.mult)
+        tt(sub(f3, 2 * K, 3 * K), nw, t2, A.is_equal)
         tt(sa, sm, Gb, A.add)
-        tt(Pm, sub(f3, K, 3 * K), dq, A.mult)
+        tt(qd, dq, s2, A.mult)
         osa, ok = V("oa%d" % n), V("ok%d" % n)
         su, oa = sub(osa, 0, K), sub(osa, K, 2 * K)
         cp(osa, sa)
         send("a", oa)
+        tt(qe, qt, gq, A.add)
+        tt(Pm, sub(f3, K, 3 * K), qd, A.mult)
+        tt(Pe, sub(f3, K, 3 * K), qe, A.mult)
+        scan(sub(sc2, 0, C), V("c16", 0, C), sub(nq, 0, C), 0.0, A.add, A.max)
         tt(P0, sub(Pe, 0, K), sub(Pe, K, 2 * K), A.add)
-        scan(sc2, V("c16"), nq, 0.0, A.add, A.max)
-        nqw, fq, km = [new("wf", 2 * K) for _ in range(3)]
+        scan(sub(sc2, C, 2 * C), V("c16", C, 2 * C), sub(nq, C, 2 * C), 0.0, A.add, A.max)
+        nqw, km = new("wf", 2 * K), new("wf", 2 * K)
         ts(nqw, (sc2[0], sc2[1] + 15, sc2[2], 16), off16, A.subtract, 2.0, A.not_equal)
-        tt(fq, nqw, tq, A.not_equal)
-        tt(km, fq, Pm, A.mult)
+        tt(km, nqw, Pm, A.mult)
         ke, kf = new("wf", K), new("wf", K)
         tt(ke, sub(km, 0, K), sub(km, K, 2 * K), A.add)
         tt(kf, ke, P0, A.add)
@@ -470,11 +465,12 @@ def rank_program(g, core, T, topo):
         else:
             pick("S", V("kr"), iof, ok)
             store("Y", [(T.co[:, :], V("kr"), T.kr[0:128:16, :])], "dz")
+        cp(tn[2], pa[2])
         if not last:
             t1, tx, t3, t4, PQ, PQG = [R() for _ in range(6)]
             wu, Gb, Gu = ties(ckR, GpR)
         for b in range(4):
-            pb = V("pb", 512 * (b % 2), 512 * (b % 2) + C)
+            pb = V("pb", 512 * (b % 3), 512 * (b % 3) + C)
             mx(pb, E4[0][b], E4[1][b], V("lq%d" % n), V("lp%d" % n))
             if b == 3:
                 ts(hn[b], pb, 0.5, A.mult)
@@ -487,16 +483,19 @@ def rank_program(g, core, T, topo):
         for b in range(4):
             ttg(V("z%d" % n, b, 4 * C, 4), hn[b], V("lk%d" % n), gn[b], A.add)
         quant(V("zq%d" % n), V("zs%d" % n), V("z%d" % n))
-        if n == 0:
-            for b in (2, 3):
-                cp(tn[b], pa[b])
-        for b in range(4):
-            mx(pa[b], V("wq", 128 * b, 128 * b + 128), V("wp", 128 * b, 128 * b + 128), V("zq%d" % n), V("zs%d" % n))
+        zq, zs, rh = "zq%d" % n, "zs%d" % n, [sub(pa[0], 0, H), V("pb", 0, H)]
+        for i in range(2):
+            mx(rh[i], V("wq", 0, 128), V("wp", 0, 128), V(zq, H * i, H * i + H), V(zs, H * i, H * i + H))
         if not last:
             lists, t2, dd = pairs(Gb)
             pick("S", tx, t1, su)
             pick("S", t3, tx, Gu)
-        for b in range(4):
+        act(tn[3], pa[3])
+        for b in range(1, 4):
+            mx(pa[b], V("wq", 128 * b, 128 * b + 128), V("wp", 128 * b, 128 * b + 128), V(zq), V(zs))
+        act(sub(rn[0], 0, H), rh[0], scale=0.03125)
+        ts(sub(rn[0], H, C), rh[1], 0.03125, A.mult)
+        for b in range(1, 4):
             act(rn[b], pa[b], scale=0.03125)
         if last:
             quant(V("vq"), V("vs"), V("vt"))
@@ -509,12 +508,13 @@ def rank_program(g, core, T, topo):
         quant(V("q%d" % (n + 1)), V("s%d" % (n + 1)), V("x%d" % (n + 1)))
 
     store("Y", [(T.oc[:, :], V("q3"), codes("q3", 0, C))], "dy")
-    store("S", [(T.osc[4 * k:4 * k + 4, :], V("s3"), T.s3[32 * k:32 * k + 4, 0:C]) for k in range(4)], "dy")
-    mx(V("pz", 0, C), V("vq"), V("vs"), V("q3"), V("s3"))
-    cp(V("yo", 0, H), V("pz", 0, H))
-    store("Y", [(T.y[:, 0:H], V("yo", 0, H), T.yo[:, 0:H])], "dy")
-    cp(V("yo", H, C), V("pz", H, C))
-    store("S", [(T.y[:, H:C], V("yo", H, C), T.yo[:, H:C])], "dy")
+    for i, bank in enumerate(("pz", "pb")):
+        mx(V(bank, 0, H), V("vq"), V("vs"), V("q3", H * i, H * i + H), V("s3", H * i, H * i + H))
+    act(V("yo", 0, H), V("pz", 0, H))
+    cp(V("yo", H, C), V("pb", 0, H))
+    for i, q in enumerate("SY"):
+        store(q, [(T.y[:, H * i:H * i + H], V("yo", H * i, H * i + H), T.yo[:, H * i:H * i + H])], "dy")
+        store(q, [(T.osc[4 * k:4 * k + 4, :], V("s3"), T.s3[32 * k:32 * k + 4, 0:C]) for k in (2 * i, 2 * i + 1)], "dy")
     for s in sorted(count):
         if known["G"].get(s, 0) < count[s]:
             g.wait_ge(T.sem[s], count[s])

from concourse.bass import DstId, RemoteDMATransfer
from concourse.mybir import dt, AluOpType, ActivationFunctionType

N = 8
C = 288
H = C // 2
K = C // 16
STEP = [1, 4, 2]
WORLD = 256
BIG, BIGF = float(2 ** 20), 4.0
A = AluOpType
COPY = ActivationFunctionType.Copy

SCRATCH = {
    "li": ("sbuf", [128, 3 * K], "int32"), "lu": ("sbuf", [128, 3 * K], "uint16"),
    "pc": ("sbuf", [128, 2], "int32"), "off": ("sbuf", [128, 4], "float32"), "iw": ("sbuf", [128, K], "float32"),
    "dd": ("sbuf", [128, C], "float32"), "sg": ("sbuf", [128, C], "float32"), "c32": ("sbuf", [128, C], "float32"), "c16": ("sbuf", [128, 2 * C], "bfloat16"),
    "io_f": ("sbuf", [128, C], "float32"), "kt": ("sbuf", [128, 2 * C], "float32"),
    "rr": ("sbuf", [128, 60 * C], "float32"), "rb": ("sbuf", [128, 30 * C], "bfloat16"),
    "wf": ("sbuf", [128, 150 * K], "float32"), "wi": ("sbuf", [128, 50 * K], "int32"), "wu": ("sbuf", [128, 40 * K], "uint16"),
    "kr": ("sbuf", [128, C], "float32"),
    "eb": ("sbuf", [128, 520], "bfloat16"), "eq": ("sbuf", [128, 512], "float8_e4m3fn_x4"), "es": ("sbuf", [128, 512], "uint8"),
    "uo_i": ("sbuf", [128, 8], "int32"), "uo": ("sbuf", [128, 8], "uint16"),
    "ut": ("sbuf", [128, 512], "bfloat16"), "uq": ("sbuf", [128, 128], "float8_e4m3fn_x4"), "us": ("sbuf", [128, 128], "uint8"),
    "pq": ("sbuf", [128, 128], "float8_e4m3fn_x4"), "pl_s": ("sbuf", [128, 128], "uint8"),
    "vt": ("sbuf", [128, 512], "bfloat16"), "vq": ("sbuf", [128, 128], "float8_e4m3fn_x4"), "vs": ("sbuf", [128, 128], "uint8"),
    "wq": ("sbuf", [128, 512], "float8_e4m3fn_x4"), "wp": ("sbuf", [128, 512], "uint8"),
    "yo": ("sbuf", [128, C], "float32"),
    "pa": ("psum", [128, 2048], "float32"), "pb": ("psum", [128, 1536], "float32"), "pz": ("psum", [128, 512], "float32"),
}
SEMAPHORES = ["sv", "ss", "sp", "sg", "dl", "du", "dx", "dw", "dv", "dy", "dz", "ls"]
for _n in range(4):
    SCRATCH["x%d" % _n] = ("sbuf", [128, 4 * C], "bfloat16")
    SCRATCH["q%d" % _n] = ("sbuf", [128, C], "float8_e4m3fn_x4")
    SCRATCH["s%d" % _n] = ("sbuf", [128, C], "uint8")
for _n in range(3):
    SCRATCH["lq%d" % _n] = ("sbuf", [128, C], "float8_e4m3fn_x4")
    SCRATCH["lp%d" % _n] = ("sbuf", [128, C], "uint8")
    SCRATCH["hq%d" % _n] = ("sbuf", [128, H], "float8_e4m3fn_x4")
    SCRATCH["hp%d" % _n] = ("sbuf", [128, H], "uint8")
    for _k in "ak":
        SCRATCH["o%s%d" % (_k, _n)] = ("sbuf", [128, 2 * K if _k == "a" else K], "uint16")
        SCRATCH["l%s%d" % (_k, _n)] = ("sbuf", [128, K], "uint16")
        for _i in range(2):
            SCRATCH["h%s%d%d" % (_k, _n, _i)] = ("sbuf", [128, K], "uint16")
            SEMAPHORES += ["h%s%d%d" % (_k, _n, _i)]
    for _k in ("t", "h", "g"):
        SCRATCH["%s%d" % (_k, _n)] = ("sbuf", [128, 4 * C], "bfloat16")
    SCRATCH["r%d" % _n] = ("sbuf", [128, 4 * C], "float32")
    SCRATCH["z%d" % _n] = ("sbuf", [128, 4 * C], "bfloat16")
    SCRATCH["zq%d" % _n] = ("sbuf", [128, C], "float8_e4m3fn_x4")
    SCRATCH["zs%d" % _n] = ("sbuf", [128, C], "uint8")
    SEMAPHORES += ["rq%d" % _n, "ra%d" % _n, "rk%d" % _n, "hq%d" % _n, "hp%d" % _n]


def routes(topo, cores):
    out, desk = [], {}
    for d in STEP:
        ends = [(cores[r], cores[(r + d) % N]) for r in range(N)]
        cross = [r for r in range(N) if not topo.may_write(*ends[r])]
        fl, taken = [None] * N, {}
        for r in reversed(cross):
            src, dst = ends[r]
            chip = topo.cores_of(src)
            alone = sum(ends[s][0] in chip for s in cross) == 1
            near, far = [], []
            for e in sorted({topo.die(k) for k in chip}, key=lambda e: e != topo.die(src))[:2 if alone else 1]:
                port = [k for k in chip if k not in cores and topo.may_write(k, dst) and topo.die(k) == e]
                near.append(port[0])
                if len(near) == 1:
                    desk.setdefault(chip[0], port[-1])
                far.append([k for k in range(WORLD) if topo.mates(k, dst) and topo.may_write(src, k) and topo.may_write(k, dst)
                            and topo.die(k) == e][0])
            out_e = topo.engines(src, far[0])
            in_e = [e for e in topo.engines(src, near[0]) if e not in out_e]
            w, parts = C // (2 * len(near)), []
            for cs, es in ((far, out_e), (near, in_e)):
                for i, k in enumerate(cs):
                    z = len(es) // len(cs)
                    a = w * len(parts)
                    parts.append((k, a, a + w, sum(1 << e for e in es[z * i:z * i + z])))
            k = desk[chip[0]]
            fl[r] = parts, (k, taken.get(k, 0))
            taken[k] = taken.get(k, 0) + 1
        out.append(fl)
    return out


def bits(m):
    return bin(m).count("1")


def rank_program(g, core, T, topo):
    cores = list(T.cores)
    ways = routes(topo, cores)
    sent = [0]

    def remote(dst, out, in_, sem):
        rid, pid = topo.addr(dst, core)
        m = topo.mask(core, dst)
        g.remote_dma(out, in_, T.sem[sem], T.sem.ls, pid, rid, m)
        sent[0] += bits(m)

    def target(dst):
        rid, pid = topo.addr(dst, core)
        return DstId(rid=rid, pnc=pid)

    def codes(name, a, b):
        return T[name][:, a:b].bitcast(dt.uint8)

    rank = T.rank_of(core)
    if rank is None:
        for n, d in enumerate(STEP):
            for r in reversed(range(N)):
                if ways[n][r] is None:
                    continue
                src, dst = cores[r], cores[(r + d) % N]
                parts, (desk, slot) = ways[n][r]
                for k, a, b, m in parts:
                    if core == k:
                        g.wait_ge(T.sem["hq%d" % n], bits(m))
                        remote(dst, codes("lq%d" % n, a, b), codes("hq%d" % n, 0, b - a), "rq%d" % n)
                        g.wait_ge(T.sem["hp%d" % n], bits(m))
                        remote(dst, T["lp%d" % n][:, a:b], T["hp%d" % n][:, 0:b - a], "rq%d" % n)
                if core == desk:
                    for k in "ak":
                        h = "h%s%d%d" % (k, n, slot)
                        g.wait_ge(T.sem[h], bits(topo.mask(src, core)))
                        remote(dst, T["l%s%d" % (k, n)][:], T[h][:], "r%s%d" % (k, n))
        if sent[0]:
            g.wait_ge(T.sem.ls, sent[0])
        return

    queue = {"V": g.vector, "S": g.scalar, "P": g.tensor, "G": g, "Y": g.sync}
    own = {"V": "sv", "S": "ss", "P": "sp", "G": "sg"}
    count, hist, snap = {}, {}, {}
    known = {q: {} for q in queue}
    top = {}

    def ap(v):
        return T[v[0]][:, v[1]:v[2]] if v[3] == 1 else T[v[0]][:, v[1]:v[2]:v[3]]

    def V(name, a=0, b=None, step=1):
        return (name, a, T[name].shape[1] if b is None else b, step)

    def new(name, n):
        a = top.get(name, 0)
        top[name] = a + n
        assert a + n <= T[name].shape[1]
        return (name, a, a + n, 1)

    def sub(v, a, b):
        return (v[0], v[1] + a, v[1] + b, 1)

    def meet(u, v):
        if u[2] <= v[1] or v[2] <= u[1]:
            return False
        return not (u[3] > 1 and u[3] == v[3] and (u[1] - v[1]) % u[3])

    def note(tok, reads, writes, seen):
        snap[tok] = dict(seen)
        snap[tok][tok[0]] = max(tok[1], snap[tok].get(tok[0], 0))
        for v in writes:
            old = hist.setdefault(v[0], [])
            hist[v[0]] = [h for h in old if not (v[3] == 1 and v[1] <= h[0][1] and h[0][2] <= v[2])] + [(v, tok, 1)]
        for v in reads:
            hist.setdefault(v[0], []).append((v, tok, 0))

    def settle(q, reads, writes):
        need = {}
        for vs, both in ((reads, False), (writes, True)):
            for v in vs:
                for h, tok, w in hist.get(v[0], []):
                    if (w or both) and meet(h, v) and known[q].get(tok[0], 0) < tok[1]:
                        need[tok[0]] = max(need.get(tok[0], 0), tok[1])
        toks = list(need.items())
        for tok in toks:
            if any(o != tok and snap[o].get(tok[0], 0) >= tok[1] for o in toks):
                continue
            queue[q].wait_ge(T.sem[tok[0]], tok[1])
        for tok in toks:
            for s, c in snap[tok].items():
                known[q][s] = max(known[q].get(s, 0), c)

    def op(q, call, reads, writes):
        settle(q, reads, writes)
        s = own[q]
        count[s] = count.get(s, 0) + 1
        call(queue[q]).then_inc(T.sem[s], 1)
        note((s, count[s]), reads, writes, known[q])

    def load(q, pairs, sem):
        settle(q, [], [v for v, _ in pairs])
        for v, src in pairs:
            side = codes(v[0], v[1], v[2]) if v[0] == "wq" else ap(v)
            queue[q].dma_start(side, src).then_inc(T.sem[sem], 16)
            count[sem] = count.get(sem, 0) + 16
        note((sem, count[sem]), [], [v for v, _ in pairs], known[q])

    def store(q, pairs, sem):
        settle(q, [v for _, v, _ in pairs], [])
        for dst, v, side in pairs:
            queue[q].dma_start(dst, side).then_inc(T.sem[sem], 16)
            count[sem] = count.get(sem, 0) + 16

    def tt(out, a, b, o):
        op("V", lambda e: e.tensor_tensor(ap(out), ap(a), ap(b), o), [a, b], [out])

    def ttg(out, win, lst, b, o):
        op("V", lambda e: e.tensor_tensor(ap(out), ap(win).indirect(ap(lst)), ap(b), o), [win, lst, b], [out])

    def ts(out, a, s1, o1, s2=None, o2=None):
        cols = [s for s in (s1, s2) if isinstance(s, tuple)]
        f = [ap(s) if isinstance(s, tuple) else s for s in (s1, s2)]
        if o2 is None:
            op("V", lambda e: e.tensor_scalar(ap(out), ap(a), f[0], None, o1), [a] + cols, [out])
        else:
            op("V", lambda e: e.tensor_scalar(ap(out), ap(a), f[0], f[1], o1, o2), [a] + cols, [out])

    def cp(out, a):
        op("V", lambda e: e.tensor_copy(ap(out), ap(a)), [a], [out])

    def act(out, a, scale=1.0, bias=0.0):
        op("S", lambda e: e.activation(ap(out), ap(a), COPY, bias=bias, scale=scale), [a], [out])

    def pick(q, out, win, lst):
        if q == "S":
            op("S", lambda e: e.activation(ap(out), ap(win).indirect(ap(lst)), COPY), [win, lst], [out])
        else:
            op("V", lambda e: e.tensor_copy(ap(out), ap(win).indirect(ap(lst))), [win, lst], [out])

    def scatter(win, lst, val):
        op("V", lambda e: e.tensor_copy(ap(win).indirect(ap(lst)), ap(val)), [lst, val], [win])

    def scan(out, d0, d1, init, o0, o1):
        op("V", lambda e: e.tensor_tensor_scan(ap(out), ap(d0), ap(d1), init, o0, o1), [d0, d1], [out])

    def quant(c, s, t):
        op("V", lambda e: e.quantize_mx(out=ap(c), scales=ap(s), in_=ap(t)), [t], [c, s])

    def mx(out, l, ls, r, rs):
        op("P", lambda e: e.matmul_mx(ap(out), ap(l), ap(ls), ap(r), ap(rs), True, True), [l, ls, r, rs], [out])

    R = lambda: new("rr", C)
    B = lambda: new("rb", C)
    off32, off16, pcf, half = V("off", 0, 1), V("off", 1, 2), V("off", 2, 3), V("off", 3, 4)
    iof, c32 = V("io_f"), V("c32")
    pc, pc15 = V("pc", 0, 1), V("pc", 1, 2)

    def table(r, *outs):
        sc = R()
        scan(sc, c32, r, 0.0, A.add, A.max)
        for o in outs:
            ts(o, (sc[0], sc[1] + 15, sc[2], 16), off32, A.subtract)

    load("Y", [(V("li", 0, K), T.cl[:]), (V("li", 2 * K, 3 * K), T.ml[:]), (V("li", K, 2 * K), T.pl[:])], "dl")
    load("S", [(V("ut"), T.u[:])], "du")
    load("Y", [(V("x0"), T.x[:])], "dx")
    op("V", lambda e: e.memset(ap(V("eb")), 1.0), [], [V("eb")])
    op("G", lambda e: e.iota(ap(pc), [[0, 1]], 0, 1), [], [pc])
    op("G", lambda e: e.iota(ap(V("dd")), [[0, K], [1, 16]], 0, 0, allow_small_or_imprecise_dtypes=True), [], [V("dd")])
    op("G", lambda e: e.iota(ap(V("uo_i")), [[16, 8]], 0, 0), [], [V("uo_i")])
    op("G", lambda e: e.iota(ap(V("iw")), [[16, K]], 0, 0, allow_small_or_imprecise_dtypes=True), [], [V("iw")])
    op("G", lambda e: e.iota(ap(iof), [[1, C]], 0, 0, allow_small_or_imprecise_dtypes=True), [], [iof])
    for i in range(2):
        v = V("kt", i * C, (i + 1) * C)
        op("G", lambda e: e.iota(ap(v), [[512, C]], i * 2 ** 18, 0, allow_small_or_imprecise_dtypes=True), [], [v])
        if i == 0:
            op("G", lambda e: e.affine_select(ap(V("eb")), ap(V("eb")), [[1, 520]], A.is_equal, 0.0, -4, -4), [V("eb")], [V("eb")])
    ts(pc15, pc, 15, A.bitwise_and)
    ts(half, pc15, -1.0, A.mult, -0.5, A.add)
    cp(pcf, pc15)
    op("S", lambda e: e.activation(ap(V("sg")), ap(V("dd")), ActivationFunctionType.Sign, bias=ap(half)), [V("dd"), half], [V("sg")])
    ts(off32, pc15, -BIG, A.mult, 15.0 * BIG, A.add)
    ts(off16, pc15, -BIGF, A.mult, 15.0 * BIGF, A.add)
    ts(c32, V("sg"), 8.5 * BIG, A.mult, -7.5 * BIG, A.add)
    for i in range(2):
        act(V("c16", i * C, i * C + C), V("sg"), scale=9.0 * BIGF, bias=-8.0 * BIGF)
    cp(V("uo"), V("uo_i"))
    lu = V("lu")
    ib, bu = new("wf", 2 * K), new("wu", K)
    ts(sub(ib, 0, K), V("iw"), pcf, A.add)
    cp(lu, V("li"))
    cu, au0, mu = sub(lu, 0, K), sub(lu, K, 2 * K), sub(lu, 2 * K, 3 * K)

    Kc, bR, cR, cj = R(), R(), R(), new("wf", 2 * K)
    ts(sub(cj, K, 2 * K), V("iw"), pcf, A.add)
    cp(sub(cj, 0, K), V("li", 0, K))
    pick("S", cR, iof, cu)
    ttg(Kc, iof, cu, V("kt", 0, C), A.add)
    scatter(bR, cu, iof)
    table(bR, bu, sub(ib, K, 2 * K))

    def links(ku):
        ckR, GpR = R(), R()
        pick("S", ckR, Kc, ku)
        pick("S", GpR, ckR, bu)
        return ckR, GpR

    def ties(ckR, GpR):
        ci, ck, gt, t, w, wf, wu = new("wi", K), new("wi", 2 * K), new("wf", 2 * K), new("wf", K), new("wf", K), new("wf", K), new("wu", K)
        gi, Gb, Gu, sc = new("wi", K), new("wi", 2 * K), new("wu", K), R()
        table(ckR, ci)
        ts(sub(ck, 0, K), ci, 511, A.bitwise_and)
        ts(sub(ck, K, 2 * K), ci, 9, A.arith_shift_right)
        scan(sc, c32, GpR, 0.0, A.add, A.max)
        tt(gt, cj, ck, A.is_gt)
        ts(gi, (sc[0], sc[1] + 15, sc[2], 16), off32, A.subtract)
        tt(t, sub(gt, 0, K), sub(gt, K, 2 * K), A.not_equal)
        ts(sub(Gb, 0, K), gi, 511, A.bitwise_and)
        ts(w, t, float(C), A.mult)
        ts(sub(Gb, K, 2 * K), gi, 9, A.arith_shift_right)
        tt(wf, w, sub(ck, 0, K), A.add)
        cp(Gu, sub(Gb, 0, K))
        cp(wu, wf)
        return wu, Gb, Gu

    def pairs(Gb):
        l, lu = new("wf", 4 * K), new("wu", 4 * K)
        g1, t2, dd = new("wf", 2 * K), new("wf", K), new("wf", 2 * K)
        tt(sub(l, 0, 2 * K), ib, Gb, A.max)
        tt(sub(l, 2 * K, 4 * K), ib, Gb, A.min)
        tt(g1, ib, Gb, A.is_gt)
        cp(lu, l)
        tt(dd, ib, Gb, A.subtract)
        tt(t2, sub(g1, 0, K), sub(g1, K, 2 * K), A.not_equal)
        return lu, t2, dd

    def cands(I):
        q, gq, t, d, hu = [new("wi", 2 * K) for _ in range(3)] + [new("wf", 2 * K), new("wu", 2 * K)]
        ts(q, I, 511, A.bitwise_and)
        ts(gq, I, 9, A.arith_shift_right, 511, A.bitwise_and)
        cp(hu, q)
        ts(t, I, 18, A.arith_shift_right)
        tt(d, q, gq, A.subtract)
        return hu, gq, t, d

    ckR, GpR = links(mu)
    quant(V("uq"), V("us"), V("ut"))
    op("S", lambda e: e.activation(T.pl_s[:, 0:128], T.us[:, 0:128].indirect(T.uo[:, 0:8]), COPY), [V("us"), V("uo")], [V("pl_s")])
    op("V", lambda e: e.tensor_copy(T.pq[:, 0:128].bitcast(dt.uint32), T.uq[:, 0:128].bitcast(dt.uint32).indirect(T.uo[:, 0:8])),
       [V("uq"), V("uo")], [V("pq")])
    quant(V("q0"), V("s0"), V("x0"))
    t1, tx, t3, t4, PQ, PQG = [R() for _ in range(6)]
    wu, Gb, Gu = ties(ckR, GpR)
    ttg(t1, V("kt"), wu, cR, A.add)
    lists, t2, dd = pairs(Gb)
    scatter(tx, au0, t1)
    settle("Y", [V("x0")], [])
    load("Y", [(V("wq"), T.wc[:]), (V("wp"), T.ws[:])], "dw")
    load("Y", [(V("vt"), T.v[:])], "dv")
    E4 = [V("eq", 128 * b, 128 * b + 128) for b in range(4)], [V("es", 128 * b, 128 * b + 128) for b in range(4)]
    P4 = lambda name: [V(name, C * b, C * b + C) for b in range(4)]

    for n, d in enumerate(STEP):
        qn, sn = V("q%d" % n), V("s%d" % n)
        dst, way = cores[(rank + d) % N], ways[n][rank]
        gr = (rank - d) % N
        gway, gsrc = ways[n][gr], cores[gr]
        last = n == 2
        settle("G", [qn, sn], [])
        if way is None:
            remote(dst, codes("lq%d" % n, 0, C), codes(qn[0], 0, C), "rq%d" % n)
            remote(dst, T["lp%d" % n][:], T[sn[0]][:], "rq%d" % n)
        else:
            for kind, piece in (("hq%d" % n, lambda a, b: (codes("hq%d" % n, 0, b - a), codes(qn[0], a, b))),
                                ("hp%d" % n, lambda a, b: (T["hp%d" % n][:, 0:b - a], T[sn[0]][:, a:b]))):
                g.remote_dma_fused([RemoteDMATransfer(dst_ids=[target(k)], dma_engine_mask=m, remote_sem=T.sem[kind],
                                                      srcs=[piece(a, b)[1]], dsts=[piece(a, b)[0]]) for k, a, b, m in way[0]],
                                   local_sem=T.sem.ls)
                sent[0] += sum(bits(m) for _, _, _, m in way[0])
        if gway is None:
            m = bits(topo.mask(gsrc, core))
            arr = {"q": 2 * m, "a": m, "k": m}
        else:
            m = bits(topo.mask(gway[1][0], core))
            arr = {"q": 2 * sum(bits(topo.mask(p[0], core)) for p in gway[0]), "a": m, "k": m}
        for k, vs in (("q", [V("lq%d" % n), V("lp%d" % n)]), ("a", [V("la%d" % n)]), ("k", [V("lk%d" % n)])):
            note(("r%s%d" % (k, n), arr[k]), [], vs, {})

        def send(k, v):
            settle("G", [v], [])
            if way is None:
                remote(dst, T["l%s%d" % (k, n)][:], ap(v), "r%s%d" % (k, n))
            else:
                h = "h%s%d%d" % (k, n, way[1][1])
                remote(way[1][0], T[h][:], ap(v), h)

        pz, pa = V("pz", 0, C), [V("pa", 512 * b, 512 * b + C) for b in range(4)]
        tn, hn, gn, rn = [P4("%s%d" % (k, n)) for k in "thgr"]
        mx(pz, V("pq"), V("pl_s"), qn, sn)
        SR, h1, h2 = R(), R(), R()
        Ab, Bb, Bc, XN, sc = [B() for _ in range(5)]
        nq, sc2 = new("rb", 2 * C), new("rb", 2 * C)
        I = new("wi", 2 * K)
        sq = new("rr", 2 * C)

        def targets():
            scan(sub(sq, 0, C), c32, PQ, 0.0, A.add, A.max)
            scan(sub(sq, C, 2 * C), c32, PQG, 0.0, A.add, A.max)
            ts(I, (sq[0], sq[1] + 15, sq[2], 16), off32, A.subtract)
            return cands(I)

        if n:
            hu, gq, tq, dq = targets()
        act(SR, pz)
        pick("S", h2, SR, sub(lists, 0, K))
        pick("S", h1, SR, sub(lists, K, 2 * K))
        ttg(Bb, SR, sub(lists, 2 * K, 3 * K), h2, A.is_ge)
        if n == 0:
            pick("S", t3, tx, mu)
        if n:
            act(Bc, Bb, bias=1.0)
        else:
            ts(Bc, Bb, 1.0, A.add)
            pick("S", t4, t3, au0)
            pick("S", PQ, t4, bu)
            pick("S", PQG, PQ, Gu)
        ttg(Ab, SR, sub(lists, 3 * K, 4 * K), h1, A.is_ge)
        scan(XN, Ab, Bc, 1.0, A.min, A.add)
        if n == 0:
            for b in range(4):
                quant(E4[0][b], E4[1][b], V("eb", 4 - b, 516 - b))
        for b in range(4):
            mx(pa[b], E4[0][b], E4[1][b], qn, sn)
        if n == 0:
            hu, gq, tq, dq = targets()
        pick("S", sub(nq, 0, C), XN, sub(hu, 0, K))
        pick("S", sub(nq, C, 2 * C), XN, sub(hu, K, 2 * K))
        for b in range(2):
            act(tn[b], pa[b])
        scan(sc, V("c16", 0, C), XN, 0.0, A.add, A.max)
        nw, f3, sm, sa = new("wf", K), new("wf", 3 * K), new("wf", 2 * K), new("wf", 2 * K)
        Pm, Pe, P0 = new("wf", 2 * K), new("wf", 2 * K), new("wf", K)
        s2, qt, qd, qe = [new("wf", 2 * K) for _ in range(4)]
        ts(nw, (sc[0], sc[1] + 15, sc[2], 16), off16, A.subtract, 2.0, A.not_equal)
        ts(s2, tq, -2.0, A.mult, 1.0, A.add)
        tt(sub(f3, 0, K), nw, t2, A.not_equal)
        tt(sub(f3, K, 2 * K), nw, t2, A.not_equal)
        tt(qt, tq, dq, A.mult)
        tt(sm, sub(f3, 0, 2 * K), dd, A.mult)
        tt(sub(f3, 2 * K, 3 * K), nw, t2, A.is_equal)
        tt(sa, sm, Gb, A.add)
        tt(qd, dq, s2, A.mult)
        osa, ok = V("oa%d" % n), V("ok%d" % n)
        su, oa = sub(osa, 0, K), sub(osa, K, 2 * K)
        cp(osa, sa)
        send("a", oa)
        tt(qe, qt, gq, A.add)
        tt(Pm, sub(f3, K, 3 * K), qd, A.mult)
        tt(Pe, sub(f3, K, 3 * K), qe, A.mult)
        scan(sub(sc2, 0, C), V("c16", 0, C), sub(nq, 0, C), 0.0, A.add, A.max)
        tt(P0, sub(Pe, 0, K), sub(Pe, K, 2 * K), A.add)
        scan(sub(sc2, C, 2 * C), V("c16", C, 2 * C), sub(nq, C, 2 * C), 0.0, A.add, A.max)
        nqw, km = new("wf", 2 * K), new("wf", 2 * K)
        ts(nqw, (sc2[0], sc2[1] + 15, sc2[2], 16), off16, A.subtract, 2.0, A.not_equal)
        tt(km, nqw, Pm, A.mult)
        ke, kf = new("wf", K), new("wf", K)
        tt(ke, sub(km, 0, K), sub(km, K, 2 * K), A.add)
        tt(kf, ke, P0, A.add)
        cp(ok, kf)
        send("k", ok)
        if not last:
            ckR, GpR = links(ok)
        else:
            pick("S", V("kr"), iof, ok)
            store("Y", [(T.co[:, :], V("kr"), T.kr[0:128:16, :])], "dz")
        cp(tn[2], pa[2])
        if not last:
            t1, tx, t3, t4, PQ, PQG = [R() for _ in range(6)]
            wu, Gb, Gu = ties(ckR, GpR)
        for b in range(4):
            pb = V("pb", 512 * (b % 3), 512 * (b % 3) + C)
            mx(pb, E4[0][b], E4[1][b], V("lq%d" % n), V("lp%d" % n))
            if b == 3:
                ts(hn[b], pb, 0.5, A.mult)
            else:
                act(hn[b], pb, scale=0.5)
        if not last:
            ttg(t1, V("kt"), wu, cR, A.add)
        for b in range(4):
            pick("S", gn[b], hn[b], V("la%d" % n))
        for b in range(4):
            ttg(V("z%d" % n, b, 4 * C, 4), hn[b], V("lk%d" % n), gn[b], A.add)
        quant(V("zq%d" % n), V("zs%d" % n), V("z%d" % n))
        zq, zs, rh = "zq%d" % n, "zs%d" % n, [sub(pa[0], 0, H), V("pb", 0, H)]
        for i in range(2):
            mx(rh[i], V("wq", 0, 128), V("wp", 0, 128), V(zq, H * i, H * i + H), V(zs, H * i, H * i + H))
        if not last:
            lists, t2, dd = pairs(Gb)
            pick("S", tx, t1, su)
            pick("S", t3, tx, Gu)
        act(tn[3], pa[3])
        for b in range(1, 4):
            mx(pa[b], V("wq", 128 * b, 128 * b + 128), V("wp", 128 * b, 128 * b + 128), V(zq), V(zs))
        act(sub(rn[0], 0, H), rh[0], scale=0.03125)
        ts(sub(rn[0], H, C), rh[1], 0.03125, A.mult)
        for b in range(1, 4):
            act(rn[b], pa[b], scale=0.03125)
        if last:
            quant(V("vq"), V("vs"), V("vt"))
        if not last:
            pick("S", t4, t3, su)
            pick("S", PQ, t4, bu)
            pick("S", PQG, PQ, Gu)
        for b in range(4):
            ttg(V("x%d" % (n + 1), b, 4 * C, 4), rn[b], oa, tn[b], A.add)
        quant(V("q%d" % (n + 1)), V("s%d" % (n + 1)), V("x%d" % (n + 1)))

    store("Y", [(T.oc[:, :], V("q3"), codes("q3", 0, C))], "dy")
    for i, bank in enumerate(("pz", "pb")):
        mx(V(bank, 0, H), V("vq"), V("vs"), V("q3", H * i, H * i + H), V("s3", H * i, H * i + H))
    act(V("yo", 0, H), V("pz", 0, H))
    cp(V("yo", H, C), V("pb", 0, H))
    for i, q in enumerate("SY"):
        store(q, [(T.y[:, H * i:H * i + H], V("yo", H * i, H * i + H), T.yo[:, H * i:H * i + H])], "dy")
        store(q, [(T.osc[4 * k:4 * k + 4, :], V("s3"), T.s3[32 * k:32 * k + 4, 0:C]) for k in (2 * i, 2 * i + 1)], "dy")
    for s in sorted(count):
        if known["G"].get(s, 0) < count[s]:
            g.wait_ge(T.sem[s], count[s])
    g.wait_ge(T.sem.ls, sent[0])
